import numpy as np
import ml_dtypes


def mxq(x, axis, fmt="e4m3"):
    dtype, down = {"e4m3": (ml_dtypes.float8_e4m3fn, 7), "e5m2": (ml_dtypes.float8_e5m2, 14)}[fmt]
    v = np.moveaxis(np.asarray(x, np.float32).astype(ml_dtypes.bfloat16).astype(np.float64), axis, -1)
    blocks = v.reshape(v.shape[:-1] + (-1, 32))
    amax = np.abs(blocks).max(-1, keepdims=True)
    byte = np.maximum(np.where(amax > 0, np.frexp(amax)[1] - 1 + 127, 0) - down, 1)
    scale = np.exp2(byte - 127.0)
    codes = (blocks / scale).astype(np.float32).astype(dtype).astype(np.float64)
    return np.moveaxis((codes * scale).reshape(v.shape), -1, axis)


WIDE = False


def mx_kscale(k):
    if not WIDE:
        return np.ones(k)
    levels = np.array([10, -10, 5, -5, 0])
    if k % 512:
        return np.exp2(np.random.permutation(np.resize(levels, k // 32))).repeat(32)
    a = np.empty((k // 512, 16))
    for p in range(k // 512):
        a[p, :8] = np.random.permutation(np.resize(levels, 8))
        for g in range(8):
            far = levels[np.abs(levels - a[p, g]) >= 10]
            a[p, g + 8] = far[np.random.randint(len(far))]
    return np.exp2(a.ravel()).repeat(32)


def f64(x):
    return np.asarray(x).astype(np.float64)


def striped(idx):
    return np.tile(idx.reshape(-1, 16).T, (8, 1)).astype(np.uint16)


def unstriped(offs):
    return offs[:16].T.reshape(-1).astype(np.int64)


E2M1 = np.array([0.0, 0.5, 1.0, 1.5, 2.0, 3.0, 4.0, 6.0, -0.0, -0.5, -1.0, -1.5, -2.0, -3.0, -4.0, -6.0])


def pack_weight(w, fmt):
    k, n = w.shape
    w = f64(np.asarray(w, np.float32).astype(ml_dtypes.bfloat16)).reshape(k // 32, 32, n)
    amax = np.abs(w).max(1)
    if fmt == "e4m3":
        byte = np.frexp(amax)[1] - 1 + 127 - 7
    else:
        mant, ex = np.frexp(amax / 6.0)
        byte = np.where(mant > 0.5, ex, ex - 1) + 127
    byte = np.clip(np.where(amax > 0, byte, 1), 1, 254)
    scaled = (w * np.exp2(127.0 - byte)[:, None, :]).reshape(k, n).astype(np.float32)
    by_word = np.ascontiguousarray(scaled.reshape(k // 512, 128, 4, n).transpose(0, 1, 3, 2))
    if fmt == "e4m3":
        words = by_word.astype(ml_dtypes.float8_e4m3fn).view(np.uint8)
    else:
        c = by_word.astype(ml_dtypes.float4_e2m1fn).view(np.uint8) & 0xF
        words = (c[..., 0::2] | (c[..., 1::2] << 4)).reshape(k // 512, 128, 2 * n)
    return np.ascontiguousarray(words), np.ascontiguousarray(byte.astype(np.uint8).reshape(k // 512, 16, n))


def unpack_weight(words, scales, fmt):
    g, _, n = scales.shape
    words = np.ascontiguousarray(words).reshape(g, 128, n, -1)
    if fmt == "e4m3":
        vals = words.view(ml_dtypes.float8_e4m3fn).astype(np.float64)
    else:
        nib = np.empty((g, 128, n, 4), np.uint8)
        nib[..., 0::2] = words & 0xF
        nib[..., 1::2] = words >> 4
        vals = E2M1[nib]
    vals = vals * np.repeat(np.exp2(scales.astype(np.float64) - 127.0), 8, axis=1)[..., None]
    return vals.transpose(0, 1, 3, 2).reshape(g * 512, n)


def gelu(v):
    return 0.5 * v * (1.0 + np.tanh(np.sqrt(2.0 / np.pi) * (v + 0.044715 * v**3)))


K, T, S, P, H = 1536, 2048, 1024, 512, 1024

def setup_inputs():
    n = np.random.standard_normal
    s = mx_kscale(K)[:, None]
    u = mx_kscale(H)[:, None]
    tab_words, tab_scales = pack_weight(n((K, T)) * s, "e4m3")
    w4_words, w4_scales = pack_weight(n((H, H)) / (u * np.sqrt(H)), "e2m1")
    order = np.random.permutation(S)
    return {
        "tab_words": tab_words, "tab_scales": tab_scales,
        "offs": striped(np.random.permutation(T)[:S]),
        "w1": (n((K, H)) / (s * np.sqrt(K))).astype(np.float32),
        "pos1": striped(order[:P]),
        "pos2": striped(order[P:]),
        "gain": (np.exp(0.3 * n(H)) * u[:, 0]).astype(np.float32),
        "w4_words": w4_words, "w4_scales": w4_scales,
    }

def reference(tab_words, tab_scales, offs, w1, pos1, pos2, gain, w4_words, w4_scales):
    v = unpack_weight(tab_words, tab_scales, "e4m3")[:, unstriped(offs)]
    w1q = mxq(f64(w1), 0, "e4m3")
    h = w1q.T @ v
    a = h[:, unstriped(pos1)]
    b = h[:, unstriped(pos2)]
    d = a - b
    z = mxq(d * f64(gain)[:, None], 0, "e4m3")
    w4 = unpack_weight(w4_words, w4_scales, "e2m1")
    y = w4.T @ z
    g = 1 / (1 + np.exp(-y))
    return b + g * d

@@ -1,0 +1,301 @@
+from contextlib import ExitStack
+
+import concourse.mybir as mybir
+from concourse.masks import make_identity
+
+K, T, S, NP, H = 1536, 2048, 1024, 512, 1024
+FLOPS = 2 * K * H * S + 2 * H * H * NP
+
+F32 = mybir.dt.float32
+BF16 = mybir.dt.bfloat16
+I32 = mybir.dt.int32
+U32 = mybir.dt.uint32
+U16 = mybir.dt.uint16
+U8 = mybir.dt.uint8
+FP8X4 = mybir.dt.float8_e4m3fn_x4
+FP4X4 = mybir.dt.float4_e2m1fn_x4
+ACT = mybir.ActivationFunctionType
+ALU = mybir.AluOpType
+
+P = 128
+CFG = {"cast1": "VSS", "diff0": "G", "z0": "GS", "chunks": [(0, 256), (256, 384), (384, 512)], "etag": {0: "endsA", 256: "zi0_0", 384: "zi1_0"}, "diff1": "GGV", "z1": ["SS", "SS", "V"], "add": "GGGGGGVV", "early": [0, 0, 0]}
+
+
+def tile_list_sensor_gated_interpolation_kernel(
+    tc, tab_words, tab_scales, offs, w1, pos1, pos2, gain, w4_words, w4_scales, out
+):
+    nc = tc.nc
+    eng = {"V": nc.vector, "G": nc.gpsimd}
+    with ExitStack() as ctx:
+        lists = ctx.enter_context(tc.tile_pool(name="lists", bufs=1))
+        keep = ctx.enter_context(tc.tile_pool(name="keep", bufs=1))
+        ring = ctx.enter_context(tc.tile_pool(name="ring", bufs=3))
+        psum = ctx.enter_context(tc.psum_pool(name="psum", bufs=8))
+
+        offs_sb = lists.tile([P, S // 16], U16, name="offs_sb")
+        pos1_sb = lists.tile([P, NP // 16], U16, name="pos1_sb")
+        pos2_sb = lists.tile([P, NP // 16], U16, name="pos2_sb")
+
+        tab_sc = keep.tile([P, T // 4], I32, name="tab_sc")
+        w4_sc = keep.tile([P, 2, H // 4], I32, name="w4_sc", align_bytes=64)
+        warm = keep.tile([P, 8], F32, name="warm")
+        nc.gpsimd.memset(tab_sc[:], 0)
+        nc.gpsimd.memset(warm[:, 0:1], 0.0)
+        nc.vector.memset(w4_sc[:], 0)
+        nc.scalar.activation(warm[:, 1:2], warm[:, 0:1], ACT.Sigmoid)
+
+        nc.sync.dma_start(offs_sb[:], offs)
+        tab_w = [keep.tile([P, T], I32, name=f"tab_w{a}") for a in range(3)]
+
+        def load_tab(a):
+            nc.sync.dma_start(tab_w[a][:], tab_words[a].rearrange("p t i -> p (t i)").bitcast(I32))
+
+        raw = {}
+
+        def load_w(a, b, m0, m1):
+            t_ = ring.tile([P, 4, 4 * (m1 - m0)], F32, name="raw", bufs=5)
+            src = w1[512 * a : 512 * (a + 1), 512 * b + 4 * m0 : 512 * b + 4 * m1]
+            nc.sync.dma_start(t_[:], src.rearrange("(p j) c -> p j c", j=4))
+            raw[a, b, m0] = t_
+
+        load_tab(0)
+        load_w(0, 0, 0, 128)
+        for q in range(4):
+            nc.sync.dma_start(tab_sc[32 * q : 32 * q + 12, :], tab_scales[:, 4 * q : 4 * q + 4, :].bitcast(I32))
+        load_tab(1)
+        load_w(1, 0, 0, 128)
+        load_tab(2)
+        load_w(2, 0, 0, 64)
+        load_w(2, 0, 64, 128)
+        nc.sync.dma_start(pos1_sb[:], pos1)
+        nc.sync.dma_start(pos2_sb[:], pos2)
+        gn = keep.tile([P, 2, 4], F32, name="gn")
+        for a in range(3):
+            load_w(a, 1, 0, 128)
+        nc.sync.dma_start(gn[:], gain.rearrange("(b p t) -> p b t", b=2, t=4))
+        w4_w = keep.tile([P, 2, 2 * H], U8, name="w4_w", align_bytes=64)
+        nc.sync.dma_start(w4_w[:].bitcast(I32), w4_words.rearrange("a p c -> p a c").bitcast(I32))
+        for q in range(4):
+            nc.sync.dma_start(
+                w4_sc[32 * q : 32 * q + 4, :, :],
+                w4_scales[:, 4 * q : 4 * q + 4, :].rearrange("a r n -> r a n").bitcast(I32),
+            )
+        ident = keep.tile([P, P], F32, name="ident")
+        make_identity(nc, ident[:])
+
+        v_sc = keep.tile([P, S], U8, name="v_sc", align_bytes=64)
+        v_w = [keep.tile([P, S], U32, name=f"v_w{a}", align_bytes=64) for a in range(3)]
+
+        def gather_tab(a):
+            nc.vector.tensor_copy(v_w[a][:], tab_w[a][:].bitcast(U32).indirect(offs_sb[:]))
+
+        grp = {}
+        ends0 = keep.tile([P, 4, 2, NP], F32, name="ends0", align_bytes=64)
+        w_c = {(a, b): keep.tile([P, 512], U32, name=f"w_c{a}{b}", align_bytes=64) for a in range(3) for b in range(2)}
+        w_s = {(a, b): keep.tile([P, 512], U8, name=f"w_s{a}{b}", align_bytes=64) for a in range(3) for b in range(2)}
+
+        def cast(e, a, b, base, m0, m1):
+            if (a, b) not in grp:
+                if b == 0:
+                    grp[a, b] = ring.tile([P, 4, P, 4], BF16, name="grp", align_bytes=64)
+                else:
+                    flat = ends0[:, a + 1, :, :].rearrange("p e j -> p (e j)").bitcast(BF16)
+                    grp[a, b] = flat.rearrange("p (t m j) -> p t m j", t=4, j=4)
+            src = raw[a, b, base][:, :, 4 * (m0 - base) : 4 * (m1 - base)].rearrange("p j (m t) -> p m j t", t=4)
+            dst = grp[a, b][:, :, m0:m1, :].rearrange("p t m j -> p m j t")
+            if e == "S":
+                nc.scalar.copy(dst, src)
+            elif e == "V":
+                nc.vector.tensor_copy(dst, src)
+            else:
+                zero = warm[:, 0:1].unsqueeze(1).unsqueeze(1).to_broadcast([P, m1 - m0, 4, 4])
+                nc.gpsimd.tensor_tensor(dst, src, zero, ALU.add)
+
+        def quant_w(a, b, t0, t1):
+            nc.vector.quantize_mx(
+                out=w_c[a, b][:, P * t0 : P * t1].bitcast(FP8X4),
+                scales=w_s[a, b][:, P * t0 : P * t1],
+                in_=grp[a, b][:, t0:t1, :, :].rearrange("p t m j -> p (t m j)"),
+            )
+
+        gather_tab(0)
+        nc.vector.tensor_copy(v_sc[:], tab_sc[:].bitcast(U8).indirect(offs_sb[:]))
+        cast("S", 0, 0, 0, 0, 128)
+        quant_w(0, 0, 0, 4)
+        gather_tab(1)
+        cast("S", 1, 0, 0, 0, 128)
+        quant_w(1, 0, 0, 4)
+        gather_tab(2)
+        cast("S", 2, 0, 0, 0, 64)
+        cast("S", 2, 0, 64, 64, 84)
+        cast("V", 2, 0, 64, 84, 128)
+        for t in range(4):
+            quant_w(2, 0, t, t + 1)
+
+        h = {(b, t): keep.tile([P, S], F32, name=f"h{b}{t}") for b in range(2) for t in range(4)}
+
+        def states(b, t, evac):
+            banks = [psum.tile([P, 512], F32, name="bank") for s in range(2)]
+            for a in range(3):
+                for s in range(2):
+                    cols = slice(512 * s, 512 * (s + 1))
+                    nc.tensor.matmul_mx(
+                        out=banks[s][:],
+                        lhsT=w_c[a, b][:, P * t : P * (t + 1)].bitcast(FP8X4),
+                        lhsT_scale=w_s[a, b][:, P * t : P * (t + 1)],
+                        rhs=v_w[a][:, cols].bitcast(FP8X4),
+                        rhs_scale=v_sc[4 * a : P, cols],
+                        start=(a == 0),
+                        stop=(a == 2),
+                    )
+            for s in range(2):
+                cols = slice(512 * s, 512 * (s + 1))
+                if evac[s] == "S":
+                    nc.scalar.copy(h[b, t][:, cols], banks[s][:])
+                else:
+                    nc.vector.tensor_copy(h[b, t][:, cols], banks[s][:])
+
+        def cast_b1(a):
+            e = CFG["cast1"][a]
+            n = 4 if e == "S" else 1
+            for i in range(n):
+                cast(e, a, 1, 0, i * P // n, (i + 1) * P // n)
+
+        ea, eb, dd = {}, {}, {}
+
+        def chunk_tiles(b, j0, j1):
+            if b == 0:
+                ends = ends0
+            else:
+                ends = keep.tile([P, 4, 2, j1 - j0], F32, name=f"ends{j0}", tag=CFG["etag"][j0], align_bytes=64)
+            ea[b, j0] = ends[:, :, 0, :]
+            eb[b, j0] = ends[:, :, 1, :]
+            dd[b, j0] = keep.tile([P, 4, j1 - j0], F32, name=f"dd{b}_{j0}")
+
+        def gather(b, t, j0, j1):
+            nc.vector.tensor_copy(ea[b, j0][:, t, :], h[b, t][:].indirect(pos1_sb[:, j0 // 16 : j1 // 16]))
+            nc.vector.tensor_copy(eb[b, j0][:, t, :], h[b, t][:].indirect(pos2_sb[:, j0 // 16 : j1 // 16]))
+
+        def diff(e, b, j0, t0, t1):
+            eng[e].tensor_tensor(dd[b, j0][:, t0:t1, :], ea[b, j0][:, t0:t1, :], eb[b, j0][:, t0:t1, :], ALU.subtract)
+
+        z_c, z_s = {}, {}
+
+        zps = {}
+
+        def weigh(e, b, j0, j1, t0, t1):
+            n = j1 - j0
+            if (b, j0) not in zps:
+                zps[b, j0] = keep.tile([P, 4, n], BF16, name=f"zp{b}_{j0}")
+            zp = zps[b, j0]
+            if e == "S":
+                for t in range(t0, t1):
+                    nc.scalar.activation(zp[:, t, :], dd[b, j0][:, t, :], ACT.Copy, scale=gn[:, b, t : t + 1])
+            else:
+                g_b = gn[:, b, t0:t1].unsqueeze(2).to_broadcast([P, t1 - t0, n])
+                eng[e].tensor_tensor(zp[:, t0:t1, :], dd[b, j0][:, t0:t1, :], g_b, ALU.mult)
+
+        def make_z(mode, b, j0, j1):
+            n = j1 - j0
+            zi = keep.tile([P, n, 4], BF16, name=f"zi{b}_{j0}", tag=f"zi{b}_{j0}", align_bytes=64)
+            if mode in ("V", "G"):
+                eng[mode].tensor_tensor(
+                    zi[:],
+                    dd[b, j0][:].rearrange("p t j -> p j t"),
+                    gn[:, b : b + 1, :].to_broadcast([P, n, 4]),
+                    ALU.mult,
+                )
+            else:
+                if (b, j0) not in zps:
+                    weigh(mode[0], b, j0, j1, 0, 4)
+                zp = zps[b, j0]
+                dst = zi[:].rearrange("p (c i) t -> p c t i", i=4)
+                src = zp[:].rearrange("p t (c i) -> p c t i", i=4)
+                if mode[1] == "V":
+                    nc.vector.tensor_copy(dst, src)
+                else:
+                    nc.scalar.copy(dst, src)
+            z_c[b, j0] = keep.tile([P, n], U32, name=f"z_c{b}_{j0}", align_bytes=64)
+            z_s[b, j0] = keep.tile([P, n], U8, name=f"z_s{b}_{j0}", align_bytes=64)
+            nc.vector.quantize_mx(
+                out=z_c[b, j0][:].bitcast(FP8X4), scales=z_s[b, j0][:], in_=zi[:].rearrange("p j t -> p (j t)")
+            )
+
+        def where(b, q):
+            j0 = 0 if b == 0 else max(c[0] for c in CFG["chunks"] if c[0] <= P * q)
+            return (b, j0), P * q - j0
+
+        def view(tiles, b, q):
+            key, c0 = where(b, q)
+            return tiles[key][:, :, c0 : c0 + P]
+
+        def gate(q):
+            res = []
+            ys = [psum.tile([P, 512], F32, name="bank") for nb in range(2)]
+            for nb in range(2):
+                for b in range(2):
+                    key, c0 = where(b, q)
+                    nc.tensor.matmul_mx(
+                        out=ys[nb][:],
+                        lhsT=z_c[key][:, c0 : c0 + P].bitcast(FP8X4),
+                        lhsT_scale=z_s[key][:, c0 : c0 + P],
+                        rhs=w4_w[:, b, 1024 * nb : 1024 * (nb + 1)].bitcast(FP4X4),
+                        rhs_scale=w4_sc[:, b, P * nb : P * (nb + 1)].bitcast(U8),
+                        start=(b == 0),
+                        stop=(b == 1),
+                    )
+            for nb in range(2):
+                g_t = ring.tile([P, 4, P], F32, name="g_t")
+                nc.scalar.activation(g_t[:], ys[nb][:].rearrange("p (m t) -> p t m", t=4), ACT.Sigmoid)
+                g_ps = psum.tile([P, 512], F32, name="bank")
+                for t in range(4):
+                    nc.tensor.transpose(g_ps[:, P * t : P * (t + 1)], g_t[:, t, :], ident[:])
+                res.append(g_ps)
+            return res
+
+        def finish(q, g_banks):
+            for nb in range(2):
+                gd = ring.tile([P, 4, P], F32, name="gd")
+                nc.vector.tensor_tensor(
+                    gd[:], g_banks[nb][:].rearrange("p (t j) -> p t j", t=4), view(dd, nb, q), ALU.mult
+                )
+                res = ring.tile([P, 4, P], F32, name="res")
+                eng[CFG["add"][2 * q + nb]].tensor_tensor(res[:], gd[:], view(eb, nb, q), ALU.add)
+                dst = out[512 * nb : 512 * (nb + 1), P * q : P * (q + 1)].rearrange("(p t) j -> p t j", t=4)
+                nc.sync.dma_start(dst, res[:])
+
+        states(0, 0, "SV")
+        cast_b1(0)
+        for t in range(1, 4):
+            states(0, t, "SS")
+        cast_b1(1)
+        cast_b1(2)
+        chunk_tiles(0, 0, NP)
+        for t in range(4):
+            gather(0, t, 0, NP)
+            if t < 3:
+                quant_w(t, 1, 0, 4)
+            diff(CFG["diff0"], 0, 0, t, t + 1)
+            weigh(CFG["z0"][0], 0, 0, NP, t, t + 1)
+        for t in range(4):
+            states(1, t, "SS")
+        make_z(CFG["z0"], 0, 0, NP)
+        gates = []
+        for i, (j0, j1) in enumerate(CFG["chunks"]):
+            chunk_tiles(1, j0, j1)
+            mode = CFG["z1"][i]
+            for t in range(4):
+                gather(1, t, j0, j1)
+                if j1 - j0 > P:
+                    diff(CFG["diff1"][i], 1, j0, t, t + 1)
+                    weigh(mode[0], 1, j0, j1, t, t + 1)
+            if j1 - j0 == P:
+                diff(CFG["diff1"][i], 1, j0, 0, 4)
+            make_z(mode, 1, j0, j1)
+            for item in gates[: CFG["early"][i]]:
+                finish(*item)
+            gates = gates[CFG["early"][i] :]
+            for q in range(j0 // P, j1 // P):
+                gates.append((q, gate(q)))
+        for item in gates:
+            finish(*item)

@@ -18,7 +18,7 @@ ACT = mybir.ActivationFunctionType
 ALU = mybir.AluOpType
 
 P = 128
-CFG = {"cast1": "VSS", "diff0": "G", "z0": "GS", "chunks": [(0, 256), (256, 384), (384, 512)], "etag": {0: "endsA", 256: "zi0_0", 384: "zi1_0"}, "diff1": "GGV", "z1": ["SS", "SS", "V"], "add": "GGGGGGVV", "early": [0, 0, 0]}
+CFG = {"cast1": "VSS", "diff0": "V", "z0": "SS", "chunks": [(0, 256), (256, 384), (384, 512)], "etag": {0: "endsA", 256: "zi0_0", 384: "zi1_0"}, "diff1": "VVV", "z1": ["SS", "SS", "SS"], "add": "VVVVVVVV"}
 
 
 def tile_list_sensor_gated_interpolation_kernel(
@@ -264,37 +264,49 @@ def tile_list_sensor_gated_interpolation_kernel(
                 dst = out[512 * nb : 512 * (nb + 1), P * q : P * (q + 1)].rearrange("(p t) j -> p t j", t=4)
                 nc.sync.dma_start(dst, res[:])
 
-        states(0, 0, "SV")
         cast_b1(0)
-        for t in range(1, 4):
+        quant_w(0, 1, 0, 4)
+        for t in range(4):
             states(0, t, "SS")
         cast_b1(1)
         cast_b1(2)
         chunk_tiles(0, 0, NP)
+
+        def settle(b, j0, j1, t0, t1, e, w):
+            diff(e, b, j0, t0, t1)
+            weigh(w, b, j0, j1, t0, t1)
+
+        late = []
         for t in range(4):
             gather(0, t, 0, NP)
-            if t < 3:
-                quant_w(t, 1, 0, 4)
-            diff(CFG["diff0"], 0, 0, t, t + 1)
-            weigh(CFG["z0"][0], 0, 0, NP, t, t + 1)
+            for item in late:
+                settle(*item)
+            late = [(0, 0, NP, t, t + 1, CFG["diff0"], CFG["z0"][0])]
+            if t < 2:
+                quant_w(t + 1, 1, 0, 4)
         for t in range(4):
             states(1, t, "SS")
-        make_z(CFG["z0"], 0, 0, NP)
         gates = []
+        zlate = [(CFG["z0"], 0, 0, NP)]
         for i, (j0, j1) in enumerate(CFG["chunks"]):
             chunk_tiles(1, j0, j1)
             mode = CFG["z1"][i]
             for t in range(4):
                 gather(1, t, j0, j1)
+                for item in late:
+                    settle(*item)
+                late = []
+                for item in zlate:
+                    make_z(*item)
+                zlate = []
                 if j1 - j0 > P:
-                    diff(CFG["diff1"][i], 1, j0, t, t + 1)
-                    weigh(mode[0], 1, j0, j1, t, t + 1)
+                    late = [(1, j0, j1, t, t + 1, CFG["diff1"][i], mode[0])]
             if j1 - j0 == P:
-                diff(CFG["diff1"][i], 1, j0, 0, 4)
+                late = [(1, j0, j1, 0, 4, CFG["diff1"][i], mode[0])]
+            for item in late:
+                settle(*item)
+            late = []
             make_z(mode, 1, j0, j1)
-            for item in gates[: CFG["early"][i]]:
-                finish(*item)
-            gates = gates[CFG["early"][i] :]
             for q in range(j0 // P, j1 // P):
                 gates.append((q, gate(q)))
         for item in gates:

@@ -18,7 +18,7 @@ ACT = mybir.ActivationFunctionType
 ALU = mybir.AluOpType
 
 P = 128
-CFG = {"cast1": "VSS", "diff0": "V", "z0": "SS", "chunks": [(0, 256), (256, 384), (384, 512)], "etag": {0: "endsA", 256: "zi0_0", 384: "zi1_0"}, "diff1": "VVV", "z1": ["SS", "SS", "SS"], "add": "VVVVVVVV"}
+CFG = {"loads": "0sa12b", "c10": 64, "ev0": "SV", "c01": -1, "c11": 1, "g01": "h00", "cast1": "VSS", "diff0": "G", "w0": "SSGG", "z0": [(0,256,"SS",-1),(256,512,"SS",0)], "ztag": {(0,256): "zi1_0"}, "chunks": [(0, 256), (256, 384), (384, 512)], "etag": {0: "endsA", 256: "zi0_0", 384: "zp1_0"}, "diff1": "GVV", "z1": ["SS","SS","V"], "add": "GGGVVVVV", "cut": (64,84), "cut0": 64, "early": [0,0,0,0]}
 
 
 def tile_list_sensor_gated_interpolation_kernel(
@@ -45,7 +45,9 @@ def tile_list_sensor_gated_interpolation_kernel(
         nc.scalar.activation(warm[:, 1:2], warm[:, 0:1], ACT.Sigmoid)
 
         nc.sync.dma_start(offs_sb[:], offs)
-        tab_w = [keep.tile([P, T], I32, name=f"tab_w{a}") for a in range(3)]
+        nc.sync.dma_start(pos1_sb[:], pos1)
+        nc.sync.dma_start(pos2_sb[:], pos2)
+        tab_w = [keep.tile([P, T], I32, name=f"tab_w{a}", tag=f"big{a}", align_bytes=64) for a in range(3)]
 
         def load_tab(a):
             nc.sync.dma_start(tab_w[a][:], tab_words[a].rearrange("p t i -> p (t i)").bitcast(I32))
@@ -53,27 +55,29 @@ def tile_list_sensor_gated_interpolation_kernel(
         raw = {}
 
         def load_w(a, b, m0, m1):
-            t_ = ring.tile([P, 4, 4 * (m1 - m0)], F32, name="raw", bufs=5)
+            t_ = ring.tile([P, 4, 4 * (m1 - m0)], F32, name="raw", bufs=6)
             src = w1[512 * a : 512 * (a + 1), 512 * b + 4 * m0 : 512 * b + 4 * m1]
             nc.sync.dma_start(t_[:], src.rearrange("(p j) c -> p j c", j=4))
             raw[a, b, m0] = t_
 
-        load_tab(0)
-        load_w(0, 0, 0, 128)
-        for q in range(4):
-            nc.sync.dma_start(tab_sc[32 * q : 32 * q + 12, :], tab_scales[:, 4 * q : 4 * q + 4, :].bitcast(I32))
-        load_tab(1)
-        load_w(1, 0, 0, 128)
-        load_tab(2)
-        load_w(2, 0, 0, 64)
-        load_w(2, 0, 64, 128)
-        nc.sync.dma_start(pos1_sb[:], pos1)
-        nc.sync.dma_start(pos2_sb[:], pos2)
+        for step in CFG["loads"]:
+            if step == "s":
+                for q in range(4):
+                    nc.sync.dma_start(
+                        tab_sc[32 * q : 32 * q + 12, :], tab_scales[:, 4 * q : 4 * q + 4, :].bitcast(I32)
+                    )
+            elif step in "012":
+                load_tab(int(step))
+            else:
+                load_w("ab".index(step), 0, 0, 128)
+        cut, cut2 = CFG["cut"]
+        load_w(2, 0, 0, cut)
+        load_w(2, 0, cut, 128)
         gn = keep.tile([P, 2, 4], F32, name="gn")
         for a in range(3):
             load_w(a, 1, 0, 128)
         nc.sync.dma_start(gn[:], gain.rearrange("(b p t) -> p b t", b=2, t=4))
-        w4_w = keep.tile([P, 2, 2 * H], U8, name="w4_w", align_bytes=64)
+        w4_w = keep.tile([P, 2, 2 * H], U8, name="w4_w", tag="big2", align_bytes=64)
         nc.sync.dma_start(w4_w[:].bitcast(I32), w4_words.rearrange("a p c -> p a c").bitcast(I32))
         for q in range(4):
             nc.sync.dma_start(
@@ -98,6 +102,8 @@ def tile_list_sensor_gated_interpolation_kernel(
             if (a, b) not in grp:
                 if b == 0:
                     grp[a, b] = ring.tile([P, 4, P, 4], BF16, name="grp", align_bytes=64)
+                elif a == 0 and CFG["g01"]:
+                    grp[a, b] = keep.tile([P, 4, P, 4], BF16, name="grp01", tag=CFG["g01"], align_bytes=64)
                 else:
                     flat = ends0[:, a + 1, :, :].rearrange("p e j -> p (e j)").bitcast(BF16)
                     grp[a, b] = flat.rearrange("p (t m j) -> p t m j", t=4, j=4)
@@ -123,18 +129,25 @@ def tile_list_sensor_gated_interpolation_kernel(
         cast("S", 0, 0, 0, 0, 128)
         quant_w(0, 0, 0, 4)
         gather_tab(1)
-        cast("S", 1, 0, 0, 0, 128)
-        quant_w(1, 0, 0, 4)
         gather_tab(2)
-        cast("S", 2, 0, 0, 0, 64)
-        cast("S", 2, 0, 64, 64, 84)
-        cast("V", 2, 0, 64, 84, 128)
+        cast("S", 1, 0, 0, 0, CFG["c10"])
+        if CFG["c10"] < 128:
+            cast("V", 1, 0, 0, CFG["c10"], 128)
+        quant_w(1, 0, 0, 4)
+        cast("S", 2, 0, 0, 0, CFG["cut0"])
+        if CFG["cut0"] < cut:
+            cast("V", 2, 0, 0, CFG["cut0"], cut)
+        if cut2 > cut:
+            cast("S", 2, 0, cut, cut, cut2)
+        cast("V", 2, 0, cut, cut2, 128)
         for t in range(4):
             quant_w(2, 0, t, t + 1)
 
-        h = {(b, t): keep.tile([P, S], F32, name=f"h{b}{t}") for b in range(2) for t in range(4)}
+        h = {}
 
         def states(b, t, evac):
+            tag = f"big{t - 2}" if (b == 1 and t >= 2) else f"h{b}{t}"
+            h[b, t] = keep.tile([P, S], F32, name=f"h{b}{t}", tag=tag, align_bytes=64)
             banks = [psum.tile([P, 512], F32, name="bank") for s in range(2)]
             for a in range(3):
                 for s in range(2):
@@ -157,6 +170,11 @@ def tile_list_sensor_gated_interpolation_kernel(
 
         def cast_b1(a):
             e = CFG["cast1"][a]
+            if e == "H":
+                cast("S", a, 1, 0, 0, 32)
+                cast("S", a, 1, 0, 32, 64)
+                cast("V", a, 1, 0, 64, 128)
+                return
             n = 4 if e == "S" else 1
             for i in range(n):
                 cast(e, a, 1, 0, i * P // n, (i + 1) * P // n)
@@ -170,7 +188,7 @@ def tile_list_sensor_gated_interpolation_kernel(
                 ends = keep.tile([P, 4, 2, j1 - j0], F32, name=f"ends{j0}", tag=CFG["etag"][j0], align_bytes=64)
             ea[b, j0] = ends[:, :, 0, :]
             eb[b, j0] = ends[:, :, 1, :]
-            dd[b, j0] = keep.tile([P, 4, j1 - j0], F32, name=f"dd{b}_{j0}")
+            dd[b, j0] = keep.tile([P, 4, j1 - j0], F32, name=f"dd{b}_{j0}", tag=f"dd{b}_{j0}", align_bytes=64)
 
         def gather(b, t, j0, j1):
             nc.vector.tensor_copy(ea[b, j0][:, t, :], h[b, t][:].indirect(pos1_sb[:, j0 // 16 : j1 // 16]))
@@ -186,7 +204,7 @@ def tile_list_sensor_gated_interpolation_kernel(
         def weigh(e, b, j0, j1, t0, t1):
             n = j1 - j0
             if (b, j0) not in zps:
-                zps[b, j0] = keep.tile([P, 4, n], BF16, name=f"zp{b}_{j0}")
+                zps[b, j0] = keep.tile([P, 4, n], BF16, name=f"zp{b}_{j0}", tag=f"zp{b}_{j0}", align_bytes=64)
             zp = zps[b, j0]
             if e == "S":
                 for t in range(t0, t1):
@@ -195,9 +213,10 @@ def tile_list_sensor_gated_interpolation_kernel(
                 g_b = gn[:, b, t0:t1].unsqueeze(2).to_broadcast([P, t1 - t0, n])
                 eng[e].tensor_tensor(zp[:, t0:t1, :], dd[b, j0][:, t0:t1, :], g_b, ALU.mult)
 
-        def make_z(mode, b, j0, j1):
+        def make_z(mode, b, j0, j1, base=None):
             n = j1 - j0
-            zi = keep.tile([P, n, 4], BF16, name=f"zi{b}_{j0}", tag=f"zi{b}_{j0}", align_bytes=64)
+            base = j0 if base is None else base
+            zi = keep.tile([P, n, 4], BF16, name=f"zi{b}_{j0}", tag=CFG["ztag"].get((b, j0), f"zi{b}_{j0}"), align_bytes=64)
             if mode in ("V", "G"):
                 eng[mode].tensor_tensor(
                     zi[:],
@@ -206,11 +225,9 @@ def tile_list_sensor_gated_interpolation_kernel(
                     ALU.mult,
                 )
             else:
-                if (b, j0) not in zps:
-                    weigh(mode[0], b, j0, j1, 0, 4)
-                zp = zps[b, j0]
+                zp = zps[b, base][:, :, j0 - base : j1 - base]
                 dst = zi[:].rearrange("p (c i) t -> p c t i", i=4)
-                src = zp[:].rearrange("p t (c i) -> p c t i", i=4)
+                src = zp.rearrange("p t (c i) -> p c t i", i=4)
                 if mode[1] == "V":
                     nc.vector.tensor_copy(dst, src)
                 else:
@@ -234,7 +251,8 @@ def tile_list_sensor_gated_interpolation_kernel(
             ys = [psum.tile([P, 512], F32, name="bank") for nb in range(2)]
             for nb in range(2):
                 for b in range(2):
-                    key, c0 = where(b, q)
+                    z0 = max(c[0] for c in CFG["z0"] if c[0] <= P * q)
+                    key, c0 = where(b, q) if b == 1 else ((0, z0), P * q - z0)
                     nc.tensor.matmul_mx(
                         out=ys[nb][:],
                         lhsT=z_c[key][:, c0 : c0 + P].bitcast(FP8X4),
@@ -255,40 +273,47 @@ def tile_list_sensor_gated_interpolation_kernel(
 
         def finish(q, g_banks):
             for nb in range(2):
-                gd = ring.tile([P, 4, P], F32, name="gd")
+                gd = ring.tile([P, 4, P], F32, name="gd", bufs=5)
                 nc.vector.tensor_tensor(
                     gd[:], g_banks[nb][:].rearrange("p (t j) -> p t j", t=4), view(dd, nb, q), ALU.mult
                 )
-                res = ring.tile([P, 4, P], F32, name="res")
+                res = ring.tile([P, 4, P], F32, name="res", bufs=4)
                 eng[CFG["add"][2 * q + nb]].tensor_tensor(res[:], gd[:], view(eb, nb, q), ALU.add)
                 dst = out[512 * nb : 512 * (nb + 1), P * q : P * (q + 1)].rearrange("(p t) j -> p t j", t=4)
                 nc.sync.dma_start(dst, res[:])
 
-        cast_b1(0)
-        quant_w(0, 1, 0, 4)
         for t in range(4):
-            states(0, t, "SS")
-        cast_b1(1)
+            states(0, t, CFG["ev0"] if t == 0 else "SS")
+            if t == CFG["c01"]:
+                cast_b1(0)
+            if t == CFG["c11"]:
+                cast_b1(1)
         cast_b1(2)
         chunk_tiles(0, 0, NP)
 
         def settle(b, j0, j1, t0, t1, e, w):
             diff(e, b, j0, t0, t1)
-            weigh(w, b, j0, j1, t0, t1)
+            if w != "V":
+                weigh(w, b, j0, j1, t0, t1)
 
         late = []
         for t in range(4):
             gather(0, t, 0, NP)
             for item in late:
                 settle(*item)
-            late = [(0, 0, NP, t, t + 1, CFG["diff0"], CFG["z0"][0])]
-            if t < 2:
-                quant_w(t + 1, 1, 0, 4)
+            late = [(0, 0, NP, t, t + 1, CFG["diff0"], CFG["w0"][t])]
+            if t == 0 and CFG["c01"] < 0:
+                cast_b1(0)
+            if t < 3:
+                quant_w(t, 1, 0, 4)
         for t in range(4):
             states(1, t, "SS")
         gates = []
-        zlate = [(CFG["z0"], 0, 0, NP)]
+        zlate = [(c[2], 0, c[0], c[1], 0) for c in CFG["z0"] if c[3] < 0]
         for i, (j0, j1) in enumerate(CFG["chunks"]):
+            for item in gates[: CFG["early"][i]]:
+                finish(*item)
+            gates = gates[CFG["early"][i] :]
             chunk_tiles(1, j0, j1)
             mode = CFG["z1"][i]
             for t in range(4):
@@ -307,6 +332,9 @@ def tile_list_sensor_gated_interpolation_kernel(
                 settle(*item)
             late = []
             make_z(mode, 1, j0, j1)
+            for c in CFG["z0"]:
+                if c[3] == i:
+                    make_z(c[2], 0, c[0], c[1], 0)
             for q in range(j0 // P, j1 // P):
                 gates.append((q, gate(q)))
         for item in gates:

@@ -18,324 +18,274 @@ ACT = mybir.ActivationFunctionType
 ALU = mybir.AluOpType
 
 P = 128
-CFG = {"loads": "0sa12b", "c10": 64, "ev0": "SV", "c01": -1, "c11": 1, "g01": "h00", "cast1": "VSS", "diff0": "G", "w0": "SSGG", "z0": [(0,256,"SS",-1),(256,512,"SS",0)], "ztag": {(0,256): "zi1_0"}, "chunks": [(0, 256), (256, 384), (384, 512)], "etag": {0: "endsA", 256: "zi0_0", 384: "zp1_0"}, "diff1": "GVV", "z1": ["SS","SS","V"], "add": "GGGVVVVV", "cut": (64,84), "cut0": 64, "early": [0,0,0,0]}
+BANK = 512
+PASSES = K // BANK
+MID = P // 2
+SHARE = 84
+ENDS = NP + NP + NP // 2
 
 
 def tile_list_sensor_gated_interpolation_kernel(
     tc, tab_words, tab_scales, offs, w1, pos1, pos2, gain, w4_words, w4_scales, out
 ):
     nc = tc.nc
-    eng = {"V": nc.vector, "G": nc.gpsimd}
     with ExitStack() as ctx:
         lists = ctx.enter_context(tc.tile_pool(name="lists", bufs=1))
         keep = ctx.enter_context(tc.tile_pool(name="keep", bufs=1))
-        ring = ctx.enter_context(tc.tile_pool(name="ring", bufs=3))
-        psum = ctx.enter_context(tc.psum_pool(name="psum", bufs=8))
+        psum = ctx.enter_context(tc.psum_pool(name="psum", bufs=1))
+
+        def sb(shape, dtype, name, over=None):
+            return keep.tile(shape, dtype, name=name, tag=over or name, align_bytes=64)
+
+        def bank(i, name):
+            return psum.tile([P, BANK], F32, name=name, tag=f"bank{i}")
 
         offs_sb = lists.tile([P, S // 16], U16, name="offs_sb")
         pos1_sb = lists.tile([P, NP // 16], U16, name="pos1_sb")
         pos2_sb = lists.tile([P, NP // 16], U16, name="pos2_sb")
 
-        tab_sc = keep.tile([P, T // 4], I32, name="tab_sc")
-        w4_sc = keep.tile([P, 2, H // 4], I32, name="w4_sc", align_bytes=64)
-        warm = keep.tile([P, 8], F32, name="warm")
+        tab_sc = sb([P, T // 4], I32, "tab_sc")
+        w4_sc = sb([P, 2, H // 4], I32, "w4_sc")
         nc.gpsimd.memset(tab_sc[:], 0)
-        nc.gpsimd.memset(warm[:, 0:1], 0.0)
-        nc.vector.memset(w4_sc[:], 0)
-        nc.scalar.activation(warm[:, 1:2], warm[:, 0:1], ACT.Sigmoid)
+        nc.gpsimd.memset(w4_sc[:], 0)
 
-        nc.sync.dma_start(offs_sb[:], offs)
-        nc.sync.dma_start(pos1_sb[:], pos1)
-        nc.sync.dma_start(pos2_sb[:], pos2)
-        tab_w = [keep.tile([P, T], I32, name=f"tab_w{a}", tag=f"big{a}", align_bytes=64) for a in range(3)]
+        tab_w = [sb([P, T], I32, f"tab_w{a}") for a in range(PASSES)]
+        raw = {}
+        gn = sb([P, 2, 4], F32, "gn")
+        w4_w = sb([P, 2, 2 * H], U8, "w4_w")
 
-        def load_tab(a):
+        def load_table(a):
             nc.sync.dma_start(tab_w[a][:], tab_words[a].rearrange("p t i -> p (t i)").bitcast(I32))
 
-        raw = {}
+        def load_w1(a, b):
+            for m0, m1 in ((0, MID), (MID, P)) if a == PASSES - 1 else ((0, P),):
+                raw[a, b, m0] = sb([P, 4, 4 * (m1 - m0)], F32, f"raw{a}{b}_{m0}")
+                src = w1[BANK * a : BANK * (a + 1), BANK * b + 4 * m0 : BANK * b + 4 * m1]
+                nc.sync.dma_start(raw[a, b, m0][:], src.rearrange("(p j) c -> p j c", j=4))
 
-        def load_w(a, b, m0, m1):
-            t_ = ring.tile([P, 4, 4 * (m1 - m0)], F32, name="raw", bufs=6)
-            src = w1[512 * a : 512 * (a + 1), 512 * b + 4 * m0 : 512 * b + 4 * m1]
-            nc.sync.dma_start(t_[:], src.rearrange("(p j) c -> p j c", j=4))
-            raw[a, b, m0] = t_
-
-        for step in CFG["loads"]:
-            if step == "s":
-                for q in range(4):
-                    nc.sync.dma_start(
-                        tab_sc[32 * q : 32 * q + 12, :], tab_scales[:, 4 * q : 4 * q + 4, :].bitcast(I32)
-                    )
-            elif step in "012":
-                load_tab(int(step))
-            else:
-                load_w("ab".index(step), 0, 0, 128)
-        cut, cut2 = CFG["cut"]
-        load_w(2, 0, 0, cut)
-        load_w(2, 0, cut, 128)
-        gn = keep.tile([P, 2, 4], F32, name="gn")
-        for a in range(3):
-            load_w(a, 1, 0, 128)
+        load_table(0)
+        nc.sync.dma_start(offs_sb[:], offs)
+        load_w1(0, 0)
+        for q in range(4):
+            nc.sync.dma_start(tab_sc[32 * q : 32 * q + 12, :], tab_scales[:, 4 * q : 4 * q + 4, :].bitcast(I32))
+        for a in range(1, PASSES):
+            load_table(a)
+            load_w1(a, 0)
+        nc.sync.dma_start(pos2_sb[:], pos2)
+        nc.sync.dma_start(pos1_sb[:], pos1)
         nc.sync.dma_start(gn[:], gain.rearrange("(b p t) -> p b t", b=2, t=4))
-        w4_w = keep.tile([P, 2, 2 * H], U8, name="w4_w", tag="big2", align_bytes=64)
+        for a in range(PASSES):
+            load_w1(a, 1)
         nc.sync.dma_start(w4_w[:].bitcast(I32), w4_words.rearrange("a p c -> p a c").bitcast(I32))
         for q in range(4):
             nc.sync.dma_start(
                 w4_sc[32 * q : 32 * q + 4, :, :],
                 w4_scales[:, 4 * q : 4 * q + 4, :].rearrange("a r n -> r a n").bitcast(I32),
             )
-        ident = keep.tile([P, P], F32, name="ident")
+        ident = sb([P, P], F32, "ident")
         make_identity(nc, ident[:])
 
-        v_sc = keep.tile([P, S], U8, name="v_sc", align_bytes=64)
-        v_w = [keep.tile([P, S], U32, name=f"v_w{a}", align_bytes=64) for a in range(3)]
+        v_sc = sb([P, S], U8, "v_sc")
+        v_w, sorted_w, w_c, h_ps, h = {}, {}, {}, {}, {}
+        w_s = {(a, b): sb([P, BANK], U8, f"w_s{a}{b}") for a in range(PASSES) for b in range(2)}
+        ends0 = sb([P, 4 * ENDS + NP // 2], F32, "ends0")
 
-        def gather_tab(a):
+        def gather_table(a, over=None):
+            v_w[a] = sb([P, S], U32, f"v_w{a}", over)
             nc.vector.tensor_copy(v_w[a][:], tab_w[a][:].bitcast(U32).indirect(offs_sb[:]))
 
-        grp = {}
-        ends0 = keep.tile([P, 4, 2, NP], F32, name="ends0", align_bytes=64)
-        w_c = {(a, b): keep.tile([P, 512], U32, name=f"w_c{a}{b}", align_bytes=64) for a in range(3) for b in range(2)}
-        w_s = {(a, b): keep.tile([P, 512], U8, name=f"w_s{a}{b}", align_bytes=64) for a in range(3) for b in range(2)}
-
-        def cast(e, a, b, base, m0, m1):
-            if (a, b) not in grp:
-                if b == 0:
-                    grp[a, b] = ring.tile([P, 4, P, 4], BF16, name="grp", align_bytes=64)
-                elif a == 0 and CFG["g01"]:
-                    grp[a, b] = keep.tile([P, 4, P, 4], BF16, name="grp01", tag=CFG["g01"], align_bytes=64)
-                else:
-                    flat = ends0[:, a + 1, :, :].rearrange("p e j -> p (e j)").bitcast(BF16)
-                    grp[a, b] = flat.rearrange("p (t m j) -> p t m j", t=4, j=4)
+        def cast(copy, a, b, m0, m1):
+            if (a, b) not in sorted_w and b == 0:
+                sorted_w[a, b] = sb([P, 4, P, 4], BF16, f"sorted_w{a}")
+            elif (a, b) not in sorted_w:
+                o = ENDS * (a + 1) + NP
+                flat = ends0[:, o : o + 2 * BANK].bitcast(BF16)
+                sorted_w[a, b] = flat.rearrange("p (t m j) -> p t m j", t=4, j=4)
+            base = MID if (a, b, MID) in raw and m0 >= MID else 0
             src = raw[a, b, base][:, :, 4 * (m0 - base) : 4 * (m1 - base)].rearrange("p j (m t) -> p m j t", t=4)
-            dst = grp[a, b][:, :, m0:m1, :].rearrange("p t m j -> p m j t")
-            if e == "S":
-                nc.scalar.copy(dst, src)
-            elif e == "V":
-                nc.vector.tensor_copy(dst, src)
-            else:
-                zero = warm[:, 0:1].unsqueeze(1).unsqueeze(1).to_broadcast([P, m1 - m0, 4, 4])
-                nc.gpsimd.tensor_tensor(dst, src, zero, ALU.add)
+            copy(sorted_w[a, b][:, :, m0:m1, :].rearrange("p t m j -> p m j t"), src)
 
-        def quant_w(a, b, t0, t1):
-            nc.vector.quantize_mx(
-                out=w_c[a, b][:, P * t0 : P * t1].bitcast(FP8X4),
-                scales=w_s[a, b][:, P * t0 : P * t1],
-                in_=grp[a, b][:, t0:t1, :, :].rearrange("p t m j -> p (t m j)"),
-            )
-
-        gather_tab(0)
-        nc.vector.tensor_copy(v_sc[:], tab_sc[:].bitcast(U8).indirect(offs_sb[:]))
-        cast("S", 0, 0, 0, 0, 128)
-        quant_w(0, 0, 0, 4)
-        gather_tab(1)
-        gather_tab(2)
-        cast("S", 1, 0, 0, 0, CFG["c10"])
-        if CFG["c10"] < 128:
-            cast("V", 1, 0, 0, CFG["c10"], 128)
-        quant_w(1, 0, 0, 4)
-        cast("S", 2, 0, 0, 0, CFG["cut0"])
-        if CFG["cut0"] < cut:
-            cast("V", 2, 0, 0, CFG["cut0"], cut)
-        if cut2 > cut:
-            cast("S", 2, 0, cut, cut, cut2)
-        cast("V", 2, 0, cut, cut2, 128)
-        for t in range(4):
-            quant_w(2, 0, t, t + 1)
-
-        h = {}
-
-        def states(b, t, evac):
-            tag = f"big{t - 2}" if (b == 1 and t >= 2) else f"h{b}{t}"
-            h[b, t] = keep.tile([P, S], F32, name=f"h{b}{t}", tag=tag, align_bytes=64)
-            banks = [psum.tile([P, 512], F32, name="bank") for s in range(2)]
-            for a in range(3):
-                for s in range(2):
-                    cols = slice(512 * s, 512 * (s + 1))
-                    nc.tensor.matmul_mx(
-                        out=banks[s][:],
-                        lhsT=w_c[a, b][:, P * t : P * (t + 1)].bitcast(FP8X4),
-                        lhsT_scale=w_s[a, b][:, P * t : P * (t + 1)],
-                        rhs=v_w[a][:, cols].bitcast(FP8X4),
-                        rhs_scale=v_sc[4 * a : P, cols],
-                        start=(a == 0),
-                        stop=(a == 2),
-                    )
-            for s in range(2):
-                cols = slice(512 * s, 512 * (s + 1))
-                if evac[s] == "S":
-                    nc.scalar.copy(h[b, t][:, cols], banks[s][:])
-                else:
-                    nc.vector.tensor_copy(h[b, t][:, cols], banks[s][:])
-
-        def cast_b1(a):
-            e = CFG["cast1"][a]
-            if e == "H":
-                cast("S", a, 1, 0, 0, 32)
-                cast("S", a, 1, 0, 32, 64)
-                cast("V", a, 1, 0, 64, 128)
-                return
-            n = 4 if e == "S" else 1
-            for i in range(n):
-                cast(e, a, 1, 0, i * P // n, (i + 1) * P // n)
-
-        ea, eb, dd = {}, {}, {}
-
-        def chunk_tiles(b, j0, j1):
-            if b == 0:
-                ends = ends0
-            else:
-                ends = keep.tile([P, 4, 2, j1 - j0], F32, name=f"ends{j0}", tag=CFG["etag"][j0], align_bytes=64)
-            ea[b, j0] = ends[:, :, 0, :]
-            eb[b, j0] = ends[:, :, 1, :]
-            dd[b, j0] = keep.tile([P, 4, j1 - j0], F32, name=f"dd{b}_{j0}", tag=f"dd{b}_{j0}", align_bytes=64)
-
-        def gather(b, t, j0, j1):
-            nc.vector.tensor_copy(ea[b, j0][:, t, :], h[b, t][:].indirect(pos1_sb[:, j0 // 16 : j1 // 16]))
-            nc.vector.tensor_copy(eb[b, j0][:, t, :], h[b, t][:].indirect(pos2_sb[:, j0 // 16 : j1 // 16]))
-
-        def diff(e, b, j0, t0, t1):
-            eng[e].tensor_tensor(dd[b, j0][:, t0:t1, :], ea[b, j0][:, t0:t1, :], eb[b, j0][:, t0:t1, :], ALU.subtract)
-
-        z_c, z_s = {}, {}
-
-        zps = {}
-
-        def weigh(e, b, j0, j1, t0, t1):
-            n = j1 - j0
-            if (b, j0) not in zps:
-                zps[b, j0] = keep.tile([P, 4, n], BF16, name=f"zp{b}_{j0}", tag=f"zp{b}_{j0}", align_bytes=64)
-            zp = zps[b, j0]
-            if e == "S":
-                for t in range(t0, t1):
-                    nc.scalar.activation(zp[:, t, :], dd[b, j0][:, t, :], ACT.Copy, scale=gn[:, b, t : t + 1])
-            else:
-                g_b = gn[:, b, t0:t1].unsqueeze(2).to_broadcast([P, t1 - t0, n])
-                eng[e].tensor_tensor(zp[:, t0:t1, :], dd[b, j0][:, t0:t1, :], g_b, ALU.mult)
-
-        def make_z(mode, b, j0, j1, base=None):
-            n = j1 - j0
-            base = j0 if base is None else base
-            zi = keep.tile([P, n, 4], BF16, name=f"zi{b}_{j0}", tag=CFG["ztag"].get((b, j0), f"zi{b}_{j0}"), align_bytes=64)
-            if mode in ("V", "G"):
-                eng[mode].tensor_tensor(
-                    zi[:],
-                    dd[b, j0][:].rearrange("p t j -> p j t"),
-                    gn[:, b : b + 1, :].to_broadcast([P, n, 4]),
-                    ALU.mult,
+        def quantise_w1(a, b, over=None):
+            w_c[a, b] = sb([P, BANK], U32, f"w_c{a}{b}", over)
+            for t0, t1 in ((0, 1), (1, 2), (2, 4)) if a == PASSES - 1 else ((0, 4),):
+                nc.vector.quantize_mx(
+                    out=w_c[a, b][:, P * t0 : P * t1].bitcast(FP8X4),
+                    scales=w_s[a, b][:, P * t0 : P * t1],
+                    in_=sorted_w[a, b][:, t0:t1, :, :].rearrange("p t m j -> p (t m j)"),
                 )
-            else:
-                zp = zps[b, base][:, :, j0 - base : j1 - base]
-                dst = zi[:].rearrange("p (c i) t -> p c t i", i=4)
-                src = zp.rearrange("p t (c i) -> p c t i", i=4)
-                if mode[1] == "V":
-                    nc.vector.tensor_copy(dst, src)
-                else:
-                    nc.scalar.copy(dst, src)
-            z_c[b, j0] = keep.tile([P, n], U32, name=f"z_c{b}_{j0}", align_bytes=64)
-            z_s[b, j0] = keep.tile([P, n], U8, name=f"z_s{b}_{j0}", align_bytes=64)
-            nc.vector.quantize_mx(
-                out=z_c[b, j0][:].bitcast(FP8X4), scales=z_s[b, j0][:], in_=zi[:].rearrange("p j t -> p (j t)")
+
+        def states(b):
+            for t in range(4):
+                for a in range(PASSES):
+                    for s in range(2):
+                        if a == 0:
+                            h_ps[b, t, s] = bank(2 * t + s, f"h_ps{b}{t}{s}")
+                        sensors = slice(BANK * s, BANK * (s + 1))
+                        nc.tensor.matmul_mx(
+                            out=h_ps[b, t, s][:],
+                            lhsT=w_c[a, b][:, P * t : P * (t + 1)].bitcast(FP8X4),
+                            lhsT_scale=w_s[a, b][:, P * t : P * (t + 1)],
+                            rhs=v_w[a][:, sensors].bitcast(FP8X4),
+                            rhs_scale=v_sc[4 * a : P, sensors],
+                            start=(a == 0),
+                            stop=(a == PASSES - 1),
+                        )
+
+        def copy_out(b, t, second_copy, over=None):
+            h[b, t] = sb([P, S], F32, f"h{b}{t}", over)
+            nc.scalar.copy(h[b, t][:, 0:BANK], h_ps[b, t, 0][:])
+            second_copy(h[b, t][:, BANK:S], h_ps[b, t, 1][:])
+
+        per_tile = ends0[:, 0 : 4 * ENDS].rearrange("p (t x) -> p t x", t=4)
+        end_b0, diff0, z_t0 = per_tile[:, :, 0:NP], per_tile[:, :, NP : 2 * NP], per_tile[:, :, 2 * NP :].bitcast(BF16)
+        end_b1, diff1, z_t1, z_words, z_c, z_s, y_ps, gate_ps, gated = {}, {}, {}, {}, {}, {}, {}, {}, {}
+
+        def listed(pos_sb, q):
+            return pos_sb[:, P * q // 16 : P * (q + 1) // 16]
+
+        def gather_b1(q, t, over=None):
+            if q not in end_b1:
+                end_b1[q] = sb([P, 4, P], F32, f"end_b1_{q}", over)
+            nc.vector.tensor_copy(end_b1[q][:, t, :], h[1, t][:].indirect(listed(pos2_sb, q)))
+
+        def gather_d1(q, t, over=None):
+            if q not in diff1:
+                diff1[q] = sb([P, 4, P], F32, f"diff1_{q}", over)
+            picked = h[1, t][:].indirect(listed(pos1_sb, q))
+            nc.vector.tensor_tensor(diff1[q][:, t, :], picked, end_b1[q][:, t, :], ALU.subtract)
+
+        def weigh1(q, t):
+            if q not in z_t1:
+                z_t1[q] = sb([P, 4, P], BF16, f"z_t1_{q}")
+            nc.scalar.activation(z_t1[q][:, t, :], diff1[q][:, t, :], ACT.Copy, scale=gn[:, 1, t : t + 1])
+
+        def interleave(b, q, src):
+            z_words[b, q] = sb([P, src.shape[2], 4], BF16, f"z_words{b}{q}")
+            nc.scalar.copy(
+                z_words[b, q][:].rearrange("p (c i) t -> p c t i", i=4), src.rearrange("p t (c i) -> p c t i", i=4)
             )
 
-        def where(b, q):
-            j0 = 0 if b == 0 else max(c[0] for c in CFG["chunks"] if c[0] <= P * q)
-            return (b, j0), P * q - j0
+        def quantise_z(b, q):
+            n = z_words[b, q].shape[1]
+            codes, scales = sb([P, n], U32, f"z_c{b}{q}"), sb([P, n], U8, f"z_s{b}{q}")
+            nc.vector.quantize_mx(
+                out=codes[:].bitcast(FP8X4), scales=scales[:], in_=z_words[b, q][:].rearrange("p j t -> p (j t)")
+            )
+            for i in range(n // P):
+                z_c[b, q + i], z_s[b, q + i] = codes[:, P * i : P * (i + 1)], scales[:, P * i : P * (i + 1)]
 
-        def view(tiles, b, q):
-            key, c0 = where(b, q)
-            return tiles[key][:, :, c0 : c0 + P]
+        def y_pass(q, b):
+            for n in range(2):
+                if b == 0:
+                    y_ps[q, n] = bank(2 * q + n, f"y_ps{q}{n}")
+                nc.tensor.matmul_mx(
+                    out=y_ps[q, n][:],
+                    lhsT=z_c[b, q].bitcast(FP8X4),
+                    lhsT_scale=z_s[b, q],
+                    rhs=w4_w[:, b, 2 * BANK * n : 2 * BANK * (n + 1)].bitcast(FP4X4),
+                    rhs_scale=w4_sc[:, b, P * n : P * (n + 1)].bitcast(U8),
+                    start=(b == 0),
+                    stop=(b == 1),
+                )
 
         def gate(q):
-            res = []
-            ys = [psum.tile([P, 512], F32, name="bank") for nb in range(2)]
-            for nb in range(2):
-                for b in range(2):
-                    z0 = max(c[0] for c in CFG["z0"] if c[0] <= P * q)
-                    key, c0 = where(b, q) if b == 1 else ((0, z0), P * q - z0)
-                    nc.tensor.matmul_mx(
-                        out=ys[nb][:],
-                        lhsT=z_c[key][:, c0 : c0 + P].bitcast(FP8X4),
-                        lhsT_scale=z_s[key][:, c0 : c0 + P],
-                        rhs=w4_w[:, b, 1024 * nb : 1024 * (nb + 1)].bitcast(FP4X4),
-                        rhs_scale=w4_sc[:, b, P * nb : P * (nb + 1)].bitcast(U8),
-                        start=(b == 0),
-                        stop=(b == 1),
-                    )
-            for nb in range(2):
-                g_t = ring.tile([P, 4, P], F32, name="g_t")
-                nc.scalar.activation(g_t[:], ys[nb][:].rearrange("p (m t) -> p t m", t=4), ACT.Sigmoid)
-                g_ps = psum.tile([P, 512], F32, name="bank")
+            for n in range(2):
+                turned = sb([P, 4, P], F32, f"turned{q}{n}")
+                nc.scalar.activation(turned[:], y_ps[q, n][:].rearrange("p (m t) -> p t m", t=4), ACT.Sigmoid)
+                gate_ps[q, n] = bank(2 * q + n, f"gate_ps{q}{n}")
                 for t in range(4):
-                    nc.tensor.transpose(g_ps[:, P * t : P * (t + 1)], g_t[:, t, :], ident[:])
-                res.append(g_ps)
-            return res
+                    nc.tensor.transpose(gate_ps[q, n][:, P * t : P * (t + 1)], turned[:, t, :], ident[:])
 
-        def finish(q, g_banks):
-            for nb in range(2):
-                gd = ring.tile([P, 4, P], F32, name="gd", bufs=5)
-                nc.vector.tensor_tensor(
-                    gd[:], g_banks[nb][:].rearrange("p (t j) -> p t j", t=4), view(dd, nb, q), ALU.mult
-                )
-                res = ring.tile([P, 4, P], F32, name="res", bufs=4)
-                eng[CFG["add"][2 * q + nb]].tensor_tensor(res[:], gd[:], view(eb, nb, q), ALU.add)
-                dst = out[512 * nb : 512 * (nb + 1), P * q : P * (q + 1)].rearrange("(p t) j -> p t j", t=4)
-                nc.sync.dma_start(dst, res[:])
+        def finish(q):
+            pairs = slice(P * q, P * (q + 1))
+            for n, d in enumerate((diff0[:, :, pairs], diff1[q][:])):
+                gated[n] = sb([P, 4, P], F32, f"gated{q}{n}", f"raw21_{MID * n}" if q == 3 else None)
+                nc.vector.tensor_tensor(gated[n][:], gate_ps[q, n][:].rearrange("p (t j) -> p t j", t=4), d, ALU.mult)
+            for n, b_end in enumerate((end_b0[:, :, pairs], end_b1[q][:])):
+                res = sb([P, 4, P], F32, f"res{q}{n}", f"raw{n}0_0" if q == 2 else None)
+                nc.vector.tensor_tensor(res[:], gated[n][:], b_end, ALU.add)
+                nc.sync.dma_start(out[BANK * n : BANK * (n + 1), pairs].rearrange("(p t) j -> p t j", t=4), res[:])
+
+        gather_table(0)
+        nc.vector.tensor_copy(v_sc[:], tab_sc[:].bitcast(U8).indirect(offs_sb[:]))
+        cast(nc.scalar.copy, 0, 0, 0, P)
+        quantise_w1(0, 0, over="tab_sc")
+        gather_table(1, over="sorted_w0")
+        cast(nc.scalar.copy, 1, 0, 0, MID)
+        cast(nc.vector.tensor_copy, 1, 0, MID, P)
+        quantise_w1(1, 0)
+        gather_table(2)
+        cast(nc.scalar.copy, 2, 0, 0, MID)
+        cast(nc.scalar.copy, 2, 0, MID, SHARE)
+        cast(nc.vector.tensor_copy, 2, 0, SHARE, P)
+        quantise_w1(2, 0)
+        states(0)
+        copy_out(0, 0, nc.vector.tensor_copy)
+        copy_out(0, 1, nc.scalar.copy)
 
         for t in range(4):
-            states(0, t, CFG["ev0"] if t == 0 else "SS")
-            if t == CFG["c01"]:
-                cast_b1(0)
-            if t == CFG["c11"]:
-                cast_b1(1)
-        cast_b1(2)
-        chunk_tiles(0, 0, NP)
+            if t < PASSES:
+                cast(nc.scalar.copy, t, 1, 0, MID)
+                cast(nc.scalar.copy, t, 1, MID, P)
+            if t + 2 < 4:
+                copy_out(0, t + 2, nc.scalar.copy)
+            nc.vector.tensor_copy(end_b0[:, t, :], h[0, t][:].indirect(pos2_sb[:, :]))
+            if t > 0:
+                quantise_w1(t - 1, 1)
+            if t == PASSES:
+                states(1)
+            nc.vector.tensor_tensor(diff0[:, t, :], h[0, t][:].indirect(pos1_sb[:, :]), end_b0[:, t, :], ALU.subtract)
+            nc.gpsimd.tensor_scalar(z_t0[:, t, :], diff0[:, t, :], gn[:, 0, t : t + 1], 0.0, ALU.mult, ALU.add)
 
-        def settle(b, j0, j1, t0, t1, e, w):
-            diff(e, b, j0, t0, t1)
-            if w != "V":
-                weigh(w, b, j0, j1, t0, t1)
+        for t, over in enumerate(("tab_w0", "tab_w1", "tab_w2", "sorted_w1")):
+            copy_out(1, t, nc.scalar.copy, over)
+        interleave(0, 0, z_t0[:, :, 0 : 2 * P])
 
-        late = []
         for t in range(4):
-            gather(0, t, 0, NP)
-            for item in late:
-                settle(*item)
-            late = [(0, 0, NP, t, t + 1, CFG["diff0"], CFG["w0"][t])]
-            if t == 0 and CFG["c01"] < 0:
-                cast_b1(0)
-            if t < 3:
-                quant_w(t, 1, 0, 4)
+            gather_b1(0, t)
+            gather_b1(1, t)
+            gather_d1(0, t)
+            gather_d1(1, t)
+            weigh1(0, t)
+        quantise_z(0, 0)
+        y_pass(0, 0)
+        y_pass(1, 0)
+        interleave(1, 0, z_t1[0][:])
         for t in range(4):
-            states(1, t, "SS")
-        gates = []
-        zlate = [(c[2], 0, c[0], c[1], 0) for c in CFG["z0"] if c[3] < 0]
-        for i, (j0, j1) in enumerate(CFG["chunks"]):
-            for item in gates[: CFG["early"][i]]:
-                finish(*item)
-            gates = gates[CFG["early"][i] :]
-            chunk_tiles(1, j0, j1)
-            mode = CFG["z1"][i]
-            for t in range(4):
-                gather(1, t, j0, j1)
-                for item in late:
-                    settle(*item)
-                late = []
-                for item in zlate:
-                    make_z(*item)
-                zlate = []
-                if j1 - j0 > P:
-                    late = [(1, j0, j1, t, t + 1, CFG["diff1"][i], mode[0])]
-            if j1 - j0 == P:
-                late = [(1, j0, j1, 0, 4, CFG["diff1"][i], mode[0])]
-            for item in late:
-                settle(*item)
-            late = []
-            make_z(mode, 1, j0, j1)
-            for c in CFG["z0"]:
-                if c[3] == i:
-                    make_z(c[2], 0, c[0], c[1], 0)
-            for q in range(j0 // P, j1 // P):
-                gates.append((q, gate(q)))
-        for item in gates:
-            finish(*item)
+            weigh1(1, t)
+        interleave(1, 1, z_t1[1][:])
+
+        for t in range(4):
+            gather_b1(2, t, over="z_words00")
+        quantise_z(1, 0)
+        y_pass(0, 1)
+        gate(0)
+        for t in range(4):
+            gather_d1(2, t, over="z_words10")
+        quantise_z(1, 1)
+        y_pass(1, 1)
+        for t in range(4):
+            weigh1(2, t)
+        interleave(1, 2, z_t1[2][:])
+        interleave(0, 2, z_t0[:, :, 2 * P : NP])
+        gate(1)
+        for t in range(4):
+            gather_b1(3, t, over="z_words11")
+        for t in range(4):
+            gather_d1(3, t)
+        for t in range(4):
+            weigh1(3, t)
+        interleave(1, 3, z_t1[3][:])
+        quantise_z(1, 2)
+        quantise_z(0, 2)
+        y_pass(2, 0)
+        y_pass(2, 1)
+        y_pass(3, 0)
+        gate(2)
+
+        finish(0)
+        quantise_z(1, 3)
+        y_pass(3, 1)
+        gate(3)
+        for q in range(1, 4):
+            finish(q)

@@ -21,8 +21,8 @@ P = 128
 BANK = 512
 PASSES = K // BANK
 MID = P // 2
-SHARE = 84
-ENDS = NP + NP + NP // 2
+QUARTER = 256
+ON_GPSIMD = 4
 
 
 def tile_list_sensor_gated_interpolation_kernel(
@@ -51,31 +51,46 @@ def tile_list_sensor_gated_interpolation_kernel(
 
         tab_w = [sb([P, T], I32, f"tab_w{a}") for a in range(PASSES)]
         raw = {}
-        gn = sb([P, 2, 4], F32, "gn")
+        ends0 = sb([P, 5 * NP], F32, "ends0")
+        diffs0 = sb([P, 8 * NP], F32, "diffs0")
+        under = {(2, 1): ends0[:, NP : 3 * NP], (2, 3): ends0[:, 3 * NP : 5 * NP]}
+        under.update({(1, 2): diffs0[:, 4 * NP : 8 * NP]})
+        z_raw = sb([P, 4 * NP], BF16, "z_raw")
+        gn0 = sb([P, 2, 2], F32, "gn0")
+        gn1 = sb([P, 4], F32, "gn1")
         w4_w = sb([P, 2, 2 * H], U8, "w4_w")
 
         def load_table(a):
             nc.sync.dma_start(tab_w[a][:], tab_words[a].rearrange("p t i -> p (t i)").bitcast(I32))
 
-        def load_w1(a, b):
-            for m0, m1 in ((0, MID), (MID, P)) if a == PASSES - 1 else ((0, P),):
-                raw[a, b, m0] = sb([P, 4, 4 * (m1 - m0)], F32, f"raw{a}{b}_{m0}")
-                src = w1[BANK * a : BANK * (a + 1), BANK * b + 4 * m0 : BANK * b + 4 * m1]
-                nc.sync.dma_start(raw[a, b, m0][:], src.rearrange("(p j) c -> p j c", j=4))
+        def load_w1(a, c, width=QUARTER):
+            if (a, c) in under:
+                raw[a, c] = under[a, c].rearrange("p (j c) -> p j c", j=4)
+            else:
+                raw[a, c] = sb([P, 4, width], F32, f"raw{a}{c}")[:]
+            src = w1[BANK * a : BANK * (a + 1), QUARTER * c : QUARTER * c + width]
+            nc.sync.dma_start(raw[a, c], src.rearrange("(p j) c -> p j c", j=4))
 
         load_table(0)
         nc.sync.dma_start(offs_sb[:], offs)
         load_w1(0, 0)
         for q in range(4):
             nc.sync.dma_start(tab_sc[32 * q : 32 * q + 12, :], tab_scales[:, 4 * q : 4 * q + 4, :].bitcast(I32))
-        for a in range(1, PASSES):
-            load_table(a)
-            load_w1(a, 0)
+        load_table(1)
+        load_w1(1, 0)
+        load_table(2)
+        load_w1(2, 0)
         nc.sync.dma_start(pos2_sb[:], pos2)
         nc.sync.dma_start(pos1_sb[:], pos1)
-        nc.sync.dma_start(gn[:], gain.rearrange("(b p t) -> p b t", b=2, t=4))
         for a in range(PASSES):
             load_w1(a, 1)
+        nc.sync.dma_start(gn0[:], gain[0:BANK].rearrange("(c p u) -> p c u", c=2, u=2))
+        nc.sync.dma_start(gn1[:], gain[BANK:H].rearrange("(p t) -> p t", t=4))
+        load_w1(0, 2)
+        load_w1(0, 3)
+        load_w1(1, 2, BANK)
+        load_w1(2, 2)
+        load_w1(2, 3)
         nc.sync.dma_start(w4_w[:].bitcast(I32), w4_words.rearrange("a p c -> p a c").bitcast(I32))
         for q in range(4):
             nc.sync.dma_start(
@@ -86,36 +101,44 @@ def tile_list_sensor_gated_interpolation_kernel(
         make_identity(nc, ident[:])
 
         v_sc = sb([P, S], U8, "v_sc")
-        v_w, sorted_w, w_c, h_ps, h = {}, {}, {}, {}, {}
-        w_s = {(a, b): sb([P, BANK], U8, f"w_s{a}{b}") for a in range(PASSES) for b in range(2)}
-        ends0 = sb([P, 4 * ENDS + NP // 2], F32, "ends0")
+        v_w, sorted_w, w_c, w_s, h_ps, h = {}, {}, {}, {}, {}, {}
 
         def gather_table(a, over=None):
             v_w[a] = sb([P, S], U32, f"v_w{a}", over)
             nc.vector.tensor_copy(v_w[a][:], tab_w[a][:].bitcast(U32).indirect(offs_sb[:]))
 
-        def cast(copy, a, b, m0, m1):
-            if (a, b) not in sorted_w and b == 0:
-                sorted_w[a, b] = sb([P, 4, P, 4], BF16, f"sorted_w{a}")
-            elif (a, b) not in sorted_w:
-                o = ENDS * (a + 1) + NP
-                flat = ends0[:, o : o + 2 * BANK].bitcast(BF16)
-                sorted_w[a, b] = flat.rearrange("p (t m j) -> p t m j", t=4, j=4)
-            base = MID if (a, b, MID) in raw and m0 >= MID else 0
-            src = raw[a, b, base][:, :, 4 * (m0 - base) : 4 * (m1 - base)].rearrange("p j (m t) -> p m j t", t=4)
-            copy(sorted_w[a, b][:, :, m0:m1, :].rearrange("p t m j -> p m j t"), src)
+        def cast0(copy, a, c, p0=0, p1=P, over=None):
+            if (a, c) == (2, 1):
+                sorted_w[a, c] = z_raw[:, 0 : 2 * NP].rearrange("p (u m j) -> p u m j", u=2, j=4)
+            elif (a, c) not in sorted_w:
+                sorted_w[a, c] = sb([P, 2, P, 4], BF16, f"sorted_w{a}{c}", over)
+            src = raw[a, c][:, :, 2 * p0 : 2 * p1].rearrange("p j (m i u) -> p m j i u", i=2, u=2)
+            copy(sorted_w[a, c][:, :, p0:p1, :].rearrange("p u (m i) j -> p m j i u", i=2), src)
 
-        def quantise_w1(a, b, over=None):
-            w_c[a, b] = sb([P, BANK], U32, f"w_c{a}{b}", over)
-            for t0, t1 in ((0, 1), (1, 2), (2, 4)) if a == PASSES - 1 else ((0, 4),):
-                nc.vector.quantize_mx(
-                    out=w_c[a, b][:, P * t0 : P * t1].bitcast(FP8X4),
-                    scales=w_s[a, b][:, P * t0 : P * t1],
-                    in_=sorted_w[a, b][:, t0:t1, :, :].rearrange("p t m j -> p (t m j)"),
-                )
+        def cast1(copy, a, c, t0=0, t1=4):
+            if (a, c) == (0, 2):
+                flat = diffs0[:, 2 * NP : 4 * NP].bitcast(BF16)
+                sorted_w[a, 2] = flat.rearrange("p (t m j) -> p t m j", t=4, j=4)
+            elif (a, 2) not in sorted_w:
+                sorted_w[a, 2] = sb([P, 4, P, 4], BF16, f"sorted_w{a}2")
+            src = raw[a, c].rearrange("p j (m t) -> p m j t", t=4)[:, :, :, t0:t1]
+            m0 = MID * (c - 2)
+            copy(sorted_w[a, 2][:, t0:t1, m0 : m0 + src.shape[1], :].rearrange("p t m j -> p m j t"), src)
 
-        def states(b):
-            for t in range(4):
+        def quantise_w1(a, c, t0, t1):
+            codes, scales = sb([P, P * (t1 - t0)], U32, f"w_c{a}{c}{t0}"), sb([P, P * (t1 - t0)], U8, f"w_s{a}{c}{t0}")
+            nc.vector.quantize_mx(
+                out=codes[:].bitcast(FP8X4),
+                scales=scales[:],
+                in_=sorted_w[a, c][:, t0:t1, :, :].rearrange("p t m j -> p (t m j)"),
+            )
+            for t in range(t0, t1):
+                cols = slice(P * (t - t0), P * (t - t0 + 1))
+                w_c[a, c, t], w_s[a, c, t] = codes[:, cols], scales[:, cols]
+
+        def states(c, tiles):
+            for i in tiles:
+                b, t = (1, i) if c == 2 else (0, 2 * c + i)
                 for a in range(PASSES):
                     for s in range(2):
                         if a == 0:
@@ -123,46 +146,71 @@ def tile_list_sensor_gated_interpolation_kernel(
                         sensors = slice(BANK * s, BANK * (s + 1))
                         nc.tensor.matmul_mx(
                             out=h_ps[b, t, s][:],
-                            lhsT=w_c[a, b][:, P * t : P * (t + 1)].bitcast(FP8X4),
-                            lhsT_scale=w_s[a, b][:, P * t : P * (t + 1)],
+                            lhsT=w_c[a, c, i].bitcast(FP8X4),
+                            lhsT_scale=w_s[a, c, i],
                             rhs=v_w[a][:, sensors].bitcast(FP8X4),
                             rhs_scale=v_sc[4 * a : P, sensors],
                             start=(a == 0),
                             stop=(a == PASSES - 1),
                         )
 
-        def copy_out(b, t, second_copy, over=None):
+        def copy_out(b, t, copy, over=None):
             h[b, t] = sb([P, S], F32, f"h{b}{t}", over)
-            nc.scalar.copy(h[b, t][:, 0:BANK], h_ps[b, t, 0][:])
-            second_copy(h[b, t][:, BANK:S], h_ps[b, t, 1][:])
+            for s in range(2):
+                copy(h[b, t][:, BANK * s : BANK * (s + 1)], h_ps[b, t, s][:])
 
-        per_tile = ends0[:, 0 : 4 * ENDS].rearrange("p (t x) -> p t x", t=4)
-        end_b0, diff0, z_t0 = per_tile[:, :, 0:NP], per_tile[:, :, NP : 2 * NP], per_tile[:, :, 2 * NP :].bitcast(BF16)
-        end_b1, diff1, z_t1, z_words, z_c, z_s, y_ps, gate_ps, gated = {}, {}, {}, {}, {}, {}, {}, {}, {}
+        end_b = [ends0[:, 0 : 4 * NP].rearrange("p (t j) -> p t j", t=4), sb([P, 4, NP], F32, "end_b1")[:]]
+        diff0 = diffs0[:].rearrange("p (t j) -> p t j", t=4)[:, :, 0:NP]
+        weighed0 = z_raw[:].rearrange("p (t j) -> p t j", t=4)
+        z_t0 = sb([P, 2, 4, 2 * P], BF16, "z_t0")
+        diff1, z_t1, z_words, z_c, z_s, y_ps, turned, gate_ps, gated = {}, {}, {}, {}, {}, {}, {}, {}, {}
 
-        def listed(pos_sb, q):
-            return pos_sb[:, P * q // 16 : P * (q + 1) // 16]
+        def gather_b(b, t):
+            nc.vector.tensor_copy(end_b[b][:, t, :], h[b, t][:].indirect(pos2_sb[:, :]))
 
-        def gather_b1(q, t, over=None):
-            if q not in end_b1:
-                end_b1[q] = sb([P, 4, P], F32, f"end_b1_{q}", over)
-            nc.vector.tensor_copy(end_b1[q][:, t, :], h[1, t][:].indirect(listed(pos2_sb, q)))
+        def gather_d0(t, i0=0, i1=2):
+            pairs = slice(2 * P * i0, 2 * P * i1)
+            picked = h[0, t][:].indirect(pos1_sb[:, 16 * i0 : 16 * i1])
+            nc.vector.tensor_tensor(diff0[:, t, pairs], picked, end_b[0][:, t, pairs], ALU.subtract)
 
-        def gather_d1(q, t, over=None):
-            if q not in diff1:
-                diff1[q] = sb([P, 4, P], F32, f"diff1_{q}", over)
-            picked = h[1, t][:].indirect(listed(pos1_sb, q))
-            nc.vector.tensor_tensor(diff1[q][:, t, :], picked, end_b1[q][:, t, :], ALU.subtract)
+        def weigh0(t, i0=0, i1=2):
+            pairs = slice(2 * P * i0, 2 * P * i1)
+            d = diff0[:, t, pairs]
+            factor = gn0[:, t // 2, t % 2 : t % 2 + 1]
+            nc.gpsimd.tensor_scalar(weighed0[:, t, pairs], d, factor, 0.0, ALU.mult, ALU.add)
+
+        def move_z0(c, i):
+            pairs = slice(2 * P * i, 2 * P * (i + 1))
+            for e in range(2):
+                src = weighed0[e:P:2, 2 * c : 2 * c + 2, pairs]
+                nc.sync.dma_start(z_t0[MID * c : MID * (c + 1), i, 2 * e : 2 * e + 2, :], src)
+
+        def gather_d1(q, t):
+            picked = h[1, t][:].indirect(pos1_sb[:, 8 * q : 8 * (q + 1)])
+            nc.vector.tensor_tensor(diff1[q][:, t, :], picked, end_b[1][:, t, P * q : P * (q + 1)], ALU.subtract)
 
         def weigh1(q, t):
             if q not in z_t1:
-                z_t1[q] = sb([P, 4, P], BF16, f"z_t1_{q}")
-            nc.scalar.activation(z_t1[q][:, t, :], diff1[q][:, t, :], ACT.Copy, scale=gn[:, 1, t : t + 1])
+                z_t1[q] = sb([P, 4, P], BF16, f"z_t1_{q}", "z_c10" if q == 2 else None)
+            nc.scalar.activation(z_t1[q][:, t, :], diff1[q][:, t, :], ACT.Copy, scale=gn1[:, t : t + 1])
 
         def interleave(b, q, src):
             z_words[b, q] = sb([P, src.shape[2], 4], BF16, f"z_words{b}{q}")
             nc.scalar.copy(
                 z_words[b, q][:].rearrange("p (c i) t -> p c t i", i=4), src.rearrange("p t (c i) -> p c t i", i=4)
+            )
+
+        def interleave_on_gpsimd(q, src):
+            z_words[0, q] = sb([P, src.shape[2], 4], BF16, f"z_words0{q}")
+            nc.gpsimd.tensor_scalar(z_words[0, q][:], src.rearrange("p t j -> p j t"), 1.0, 0.0, ALU.mult, ALU.add)
+
+        def weigh_and_interleave1(q):
+            z_words[1, q] = sb([P, P, 4], BF16, f"z_words1{q}")
+            nc.vector.tensor_tensor(
+                z_words[1, q][:].rearrange("p (c i) t -> p c t i", i=4),
+                diff1[q].rearrange("p t (c i) -> p c t i", i=4),
+                gn1[:].unsqueeze(1).unsqueeze(3).to_broadcast([P, P // 4, 4, 4]),
+                ALU.mult,
             )
 
         def quantise_z(b, q):
@@ -188,104 +236,126 @@ def tile_list_sensor_gated_interpolation_kernel(
                     stop=(b == 1),
                 )
 
-        def gate(q):
-            for n in range(2):
-                turned = sb([P, 4, P], F32, f"turned{q}{n}")
-                nc.scalar.activation(turned[:], y_ps[q, n][:].rearrange("p (m t) -> p t m", t=4), ACT.Sigmoid)
-                gate_ps[q, n] = bank(2 * q + n, f"gate_ps{q}{n}")
-                for t in range(4):
-                    nc.tensor.transpose(gate_ps[q, n][:, P * t : P * (t + 1)], turned[:, t, :], ident[:])
+        def sigmoid(q, n):
+            turned[q, n] = sb([P, 4, P], F32, f"turned{q}{n}")
+            if n == 0:
+                dst = turned[q, n][:].rearrange("p (c u) m -> p c u m", c=2)
+                src = y_ps[q, n][:].rearrange("p (c m u) -> p c u m", c=2, u=2)
+            else:
+                dst, src = turned[q, n][:], y_ps[q, n][:].rearrange("p (m t) -> p t m", t=4)
+            nc.scalar.activation(dst, src, ACT.Sigmoid)
 
-        def finish(q):
+        def turn(q, n):
+            gate_ps[q, n] = bank(2 * q + n, f"gate_ps{q}{n}")
+            for t in range(4):
+                nc.tensor.transpose(gate_ps[q, n][:, P * t : P * (t + 1)], turned[q, n][:, t, :], ident[:])
+
+        def product(q, n):
+            d = diff1[q] if n else diff0[:, :, P * q : P * (q + 1)]
+            gated[q, n] = sb([P, 4, P], F32, f"gated{q}{n}", ("raw00", "raw01", "raw10", "raw11", "raw20", "raw02", "sorted_w00", "raw22")[2 * q + n])
+            nc.vector.tensor_tensor(gated[q, n][:], gate_ps[q, n][:].rearrange("p (t j) -> p t j", t=4), d, ALU.mult)
+
+        def finish(engine, q, n):
             pairs = slice(P * q, P * (q + 1))
-            for n, d in enumerate((diff0[:, :, pairs], diff1[q][:])):
-                gated[n] = sb([P, 4, P], F32, f"gated{q}{n}", f"raw21_{MID * n}" if q == 3 else None)
-                nc.vector.tensor_tensor(gated[n][:], gate_ps[q, n][:].rearrange("p (t j) -> p t j", t=4), d, ALU.mult)
-            for n, b_end in enumerate((end_b0[:, :, pairs], end_b1[q][:])):
-                res = sb([P, 4, P], F32, f"res{q}{n}", f"raw{n}0_0" if q == 2 else None)
-                nc.vector.tensor_tensor(res[:], gated[n][:], b_end, ALU.add)
-                nc.sync.dma_start(out[BANK * n : BANK * (n + 1), pairs].rearrange("(p t) j -> p t j", t=4), res[:])
+            res = sb([P, 4, P], F32, f"res{q}{n}", "z_words13" if (q, n) == (0, 0) else None)
+            engine.tensor_tensor(res[:], gated[q, n][:], end_b[n][:, :, pairs], ALU.add)
+            if n:
+                nc.sync.dma_start(out[BANK:H, pairs].rearrange("(p t) j -> p t j", t=4), res[:])
+            else:
+                for c in range(2):
+                    rows = out[QUARTER * c : QUARTER * (c + 1), pairs]
+                    nc.sync.dma_start(rows.rearrange("(p u) j -> p u j", u=2), res[:, 2 * c : 2 * c + 2, :])
 
         gather_table(0)
         nc.vector.tensor_copy(v_sc[:], tab_sc[:].bitcast(U8).indirect(offs_sb[:]))
-        cast(nc.scalar.copy, 0, 0, 0, P)
-        quantise_w1(0, 0, over="tab_sc")
-        gather_table(1, over="sorted_w0")
-        cast(nc.scalar.copy, 1, 0, 0, MID)
-        cast(nc.vector.tensor_copy, 1, 0, MID, P)
-        quantise_w1(1, 0)
+        cast0(nc.scalar.copy, 0, 0)
+        quantise_w1(0, 0, 0, 2)
+        gather_table(1)
+        cast0(nc.scalar.copy, 1, 0)
+        quantise_w1(1, 0, 0, 2)
         gather_table(2)
-        cast(nc.scalar.copy, 2, 0, 0, MID)
-        cast(nc.scalar.copy, 2, 0, MID, SHARE)
-        cast(nc.vector.tensor_copy, 2, 0, SHARE, P)
-        quantise_w1(2, 0)
-        states(0)
+        cast0(nc.scalar.copy, 2, 0)
+        quantise_w1(2, 0, 0, 1)
+        quantise_w1(2, 0, 1, 2)
+        states(0, (0, 1))
+        cast0(nc.vector.tensor_copy, 0, 1, over="raw20")
+        quantise_w1(0, 1, 0, 2)
         copy_out(0, 0, nc.vector.tensor_copy)
-        copy_out(0, 1, nc.scalar.copy)
-
-        for t in range(4):
-            if t < PASSES:
-                cast(nc.scalar.copy, t, 1, 0, MID)
-                cast(nc.scalar.copy, t, 1, MID, P)
-            if t + 2 < 4:
-                copy_out(0, t + 2, nc.scalar.copy)
-            nc.vector.tensor_copy(end_b0[:, t, :], h[0, t][:].indirect(pos2_sb[:, :]))
-            if t > 0:
-                quantise_w1(t - 1, 1)
-            if t == PASSES:
-                states(1)
-            nc.vector.tensor_tensor(diff0[:, t, :], h[0, t][:].indirect(pos1_sb[:, :]), end_b0[:, t, :], ALU.subtract)
-            nc.gpsimd.tensor_scalar(z_t0[:, t, :], diff0[:, t, :], gn[:, 0, t : t + 1], 0.0, ALU.mult, ALU.add)
-
-        for t, over in enumerate(("tab_w0", "tab_w1", "tab_w2", "sorted_w1")):
+        cast0(nc.scalar.copy, 1, 1)
+        copy_out(0, 1, nc.scalar.copy, "raw11")
+        cast0(nc.scalar.copy, 2, 1)
+        gather_b(0, 0)
+        quantise_w1(1, 1, 0, 2)
+        gather_d0(0)
+        cast1(nc.scalar.copy, 0, 2)
+        cast1(nc.vector.tensor_copy, 0, 3)
+        quantise_w1(2, 1, 0, 2)
+        states(1, (0, 1))
+        weigh0(0)
+        gather_b(0, 1)
+        quantise_w1(0, 2, 0, 4)
+        gather_d0(1)
+        weigh0(1)
+        move_z0(0, 0)
+        move_z0(0, 1)
+        copy_out(0, 2, nc.scalar.copy, "raw02")
+        copy_out(0, 3, nc.scalar.copy, "raw03")
+        cast1(nc.scalar.copy, 1, 2, 0, 2)
+        cast1(nc.scalar.copy, 2, 2)
+        cast1(nc.scalar.copy, 2, 3)
+        cast1(nc.vector.tensor_copy, 1, 2, 2, 4)
+        gather_b(0, 2)
+        quantise_w1(1, 2, 0, 4)
+        gather_d0(2)
+        weigh0(2)
+        quantise_w1(2, 2, 0, 1)
+        gather_b(0, 3)
+        quantise_w1(2, 2, 1, 2)
+        quantise_w1(2, 2, 2, 4)
+        states(2, range(4))
+        for i in range(2):
+            gather_d0(3, i, i + 1)
+            weigh0(3, i, i + 1)
+            move_z0(1, i)
+        for t, over in enumerate(("tab_w0", "tab_w1", "tab_w2", "h00")):
             copy_out(1, t, nc.scalar.copy, over)
-        interleave(0, 0, z_t0[:, :, 0 : 2 * P])
-
-        for t in range(4):
-            gather_b1(0, t)
-            gather_b1(1, t)
-            gather_d1(0, t)
-            gather_d1(1, t)
-            weigh1(0, t)
+            gather_b(1, t)
+        interleave(0, 0, z_t0[:, 0, :, :])
+        interleave_on_gpsimd(2, z_t0[:, 1, :, :])
         quantise_z(0, 0)
         y_pass(0, 0)
         y_pass(1, 0)
-        interleave(1, 0, z_t1[0][:])
-        for t in range(4):
-            weigh1(1, t)
-        interleave(1, 1, z_t1[1][:])
-
-        for t in range(4):
-            gather_b1(2, t, over="z_words00")
-        quantise_z(1, 0)
-        y_pass(0, 1)
-        gate(0)
-        for t in range(4):
-            gather_d1(2, t, over="z_words10")
-        quantise_z(1, 1)
-        y_pass(1, 1)
-        for t in range(4):
-            weigh1(2, t)
-        interleave(1, 2, z_t1[2][:])
-        interleave(0, 2, z_t0[:, :, 2 * P : NP])
-        gate(1)
-        for t in range(4):
-            gather_b1(3, t, over="z_words11")
-        for t in range(4):
-            gather_d1(3, t)
-        for t in range(4):
-            weigh1(3, t)
-        interleave(1, 3, z_t1[3][:])
-        quantise_z(1, 2)
-        quantise_z(0, 2)
-        y_pass(2, 0)
-        y_pass(2, 1)
-        y_pass(3, 0)
-        gate(2)
-
-        finish(0)
-        quantise_z(1, 3)
-        y_pass(3, 1)
-        gate(3)
-        for q in range(1, 4):
-            finish(q)
+        first_two = sb([P, 2, 4, P], F32, "diff1_01", "z_t0")
+        for q in range(4):
+            diff1[q] = first_two[:, q, :, :] if q < 2 else sb([P, 4, P], F32, f"diff1_{q}", f"z_t1_{q - 2}")[:]
+            if q >= 2:
+                quantise_z(1, q - 2)
+                y_pass(q - 2, 1)
+            if q == 2:
+                sigmoid(0, 0)
+            for t in range(4):
+                gather_d1(q, t)
+                if q < 3:
+                    weigh1(q, t)
+            if q == 0:
+                quantise_z(0, 2)
+                y_pass(2, 0)
+                y_pass(3, 0)
+            if q < 3:
+                interleave(1, q, z_t1[q][:])
+        weigh_and_interleave1(3)
+        for q in (2, 3):
+            quantise_z(1, q)
+            y_pass(q, 1)
+        for q in range(4):
+            for n in range(2):
+                if (q, n) != (0, 0):
+                    sigmoid(q, n)
+                turn(q, n)
+        for q in range(4):
+            for n in range(2):
+                product(q, n)
+                if 2 * q + n < ON_GPSIMD:
+                    finish(nc.gpsimd, q, n)
+        for i in range(ON_GPSIMD, 8):
+            finish(nc.vector, i // 2, i % 2)

@@ -22,7 +22,6 @@ BANK = 512
 PASSES = K // BANK
 MID = P // 2
 QUARTER = 256
-ON_GPSIMD = 4
 
 
 def tile_list_sensor_gated_interpolation_kernel(
@@ -159,19 +158,25 @@ def tile_list_sensor_gated_interpolation_kernel(
             for s in range(2):
                 copy(h[b, t][:, BANK * s : BANK * (s + 1)], h_ps[b, t, s][:])
 
-        end_b = [ends0[:, 0 : 4 * NP].rearrange("p (t j) -> p t j", t=4), sb([P, 4, NP], F32, "end_b1")[:]]
+        end_b0 = ends0[:, 0 : 4 * NP].rearrange("p (t j) -> p t j", t=4)
         diff0 = diffs0[:].rearrange("p (t j) -> p t j", t=4)[:, :, 0:NP]
         weighed0 = z_raw[:].rearrange("p (t j) -> p t j", t=4)
-        z_t0 = sb([P, 2, 4, 2 * P], BF16, "z_t0")
+        z_t0 = [sb([P, 4, 2 * P], BF16, f"z_t0_{i}") for i in range(2)]
+        end_b1 = {}
         diff1, z_t1, z_words, z_c, z_s, y_ps, turned, gate_ps, gated = {}, {}, {}, {}, {}, {}, {}, {}, {}
 
         def gather_b(b, t):
-            nc.vector.tensor_copy(end_b[b][:, t, :], h[b, t][:].indirect(pos2_sb[:, :]))
+            nc.vector.tensor_copy(end_b0[:, t, :], h[b, t][:].indirect(pos2_sb[:, :]))
+
+        def gather_b1(q, t, over=None):
+            if q not in end_b1:
+                end_b1[q] = sb([P, 4, P], F32, f"end_b1_{q}", over)[:]
+            nc.vector.tensor_copy(end_b1[q][:, t, :], h[1, t][:].indirect(pos2_sb[:, 8 * q : 8 * (q + 1)]))
 
         def gather_d0(t, i0=0, i1=2):
             pairs = slice(2 * P * i0, 2 * P * i1)
             picked = h[0, t][:].indirect(pos1_sb[:, 16 * i0 : 16 * i1])
-            nc.vector.tensor_tensor(diff0[:, t, pairs], picked, end_b[0][:, t, pairs], ALU.subtract)
+            nc.vector.tensor_tensor(diff0[:, t, pairs], picked, end_b0[:, t, pairs], ALU.subtract)
 
         def weigh0(t, i0=0, i1=2):
             pairs = slice(2 * P * i0, 2 * P * i1)
@@ -183,34 +188,26 @@ def tile_list_sensor_gated_interpolation_kernel(
             pairs = slice(2 * P * i, 2 * P * (i + 1))
             for e in range(2):
                 src = weighed0[e:P:2, 2 * c : 2 * c + 2, pairs]
-                nc.sync.dma_start(z_t0[MID * c : MID * (c + 1), i, 2 * e : 2 * e + 2, :], src)
+                nc.sync.dma_start(z_t0[i][MID * c : MID * (c + 1), 2 * e : 2 * e + 2, :], src)
 
-        def gather_d1(q, t):
+        def gather_d1(q, t, over=None):
+            if q not in diff1:
+                diff1[q] = sb([P, 4, P], F32, f"diff1_{q}", over)[:]
             picked = h[1, t][:].indirect(pos1_sb[:, 8 * q : 8 * (q + 1)])
-            nc.vector.tensor_tensor(diff1[q][:, t, :], picked, end_b[1][:, t, P * q : P * (q + 1)], ALU.subtract)
+            nc.vector.tensor_tensor(diff1[q][:, t, :], picked, end_b1[q][:, t, :], ALU.subtract)
 
         def weigh1(q, t):
-            if q not in z_t1:
-                z_t1[q] = sb([P, 4, P], BF16, f"z_t1_{q}", "z_c10" if q == 2 else None)
+            if q == 0 and t == 0:
+                both = sb([P, 2, 4, P], BF16, "z_t1_01", "z_raw")
+                z_t1[0], z_t1[1] = both[:, 0, :, :], both[:, 1, :, :]
+            elif q not in z_t1:
+                z_t1[q] = sb([P, 4, P], BF16, f"z_t1_{q}")
             nc.scalar.activation(z_t1[q][:, t, :], diff1[q][:, t, :], ACT.Copy, scale=gn1[:, t : t + 1])
 
         def interleave(b, q, src):
             z_words[b, q] = sb([P, src.shape[2], 4], BF16, f"z_words{b}{q}")
             nc.scalar.copy(
                 z_words[b, q][:].rearrange("p (c i) t -> p c t i", i=4), src.rearrange("p t (c i) -> p c t i", i=4)
-            )
-
-        def interleave_on_gpsimd(q, src):
-            z_words[0, q] = sb([P, src.shape[2], 4], BF16, f"z_words0{q}")
-            nc.gpsimd.tensor_scalar(z_words[0, q][:], src.rearrange("p t j -> p j t"), 1.0, 0.0, ALU.mult, ALU.add)
-
-        def weigh_and_interleave1(q):
-            z_words[1, q] = sb([P, P, 4], BF16, f"z_words1{q}")
-            nc.vector.tensor_tensor(
-                z_words[1, q][:].rearrange("p (c i) t -> p c t i", i=4),
-                diff1[q].rearrange("p t (c i) -> p c t i", i=4),
-                gn1[:].unsqueeze(1).unsqueeze(3).to_broadcast([P, P // 4, 4, 4]),
-                ALU.mult,
             )
 
         def quantise_z(b, q):
@@ -257,14 +254,25 @@ def tile_list_sensor_gated_interpolation_kernel(
 
         def finish(engine, q, n):
             pairs = slice(P * q, P * (q + 1))
-            res = sb([P, 4, P], F32, f"res{q}{n}", "z_words13" if (q, n) == (0, 0) else None)
-            engine.tensor_tensor(res[:], gated[q, n][:], end_b[n][:, :, pairs], ALU.add)
+            res = sb([P, 4, P], F32, f"res{q}{n}")
+            engine.tensor_tensor(res[:], gated[q, n][:], end_b1[q] if n else end_b0[:, :, pairs], ALU.add)
             if n:
                 nc.sync.dma_start(out[BANK:H, pairs].rearrange("(p t) j -> p t j", t=4), res[:])
             else:
                 for c in range(2):
                     rows = out[QUARTER * c : QUARTER * (c + 1), pairs]
                     nc.sync.dma_start(rows.rearrange("(p u) j -> p u j", u=2), res[:, 2 * c : 2 * c + 2, :])
+
+        def gate(q):
+            for n in range(2):
+                sigmoid(q, n)
+                turn(q, n)
+
+        def finish_chunk(q):
+            for n in range(2):
+                product(q, n)
+            for n in range(2):
+                finish(nc.vector, q, n)
 
         gather_table(0)
         nc.vector.tensor_copy(v_sc[:], tab_sc[:].bitcast(U8).indirect(offs_sb[:]))
@@ -319,43 +327,53 @@ def tile_list_sensor_gated_interpolation_kernel(
             move_z0(1, i)
         for t, over in enumerate(("tab_w0", "tab_w1", "tab_w2", "h00")):
             copy_out(1, t, nc.scalar.copy, over)
-            gather_b(1, t)
-        interleave(0, 0, z_t0[:, 0, :, :])
-        interleave_on_gpsimd(2, z_t0[:, 1, :, :])
+        interleave(0, 0, z_t0[0][:])
+
+        for t in range(4):
+            gather_b1(0, t)
+            gather_b1(1, t)
+            gather_d1(0, t)
+            gather_d1(1, t)
+            weigh1(0, t)
         quantise_z(0, 0)
         y_pass(0, 0)
         y_pass(1, 0)
-        first_two = sb([P, 2, 4, P], F32, "diff1_01", "z_t0")
-        for q in range(4):
-            diff1[q] = first_two[:, q, :, :] if q < 2 else sb([P, 4, P], F32, f"diff1_{q}", f"z_t1_{q - 2}")[:]
-            if q >= 2:
-                quantise_z(1, q - 2)
-                y_pass(q - 2, 1)
-            if q == 2:
-                sigmoid(0, 0)
-            for t in range(4):
-                gather_d1(q, t)
-                if q < 3:
-                    weigh1(q, t)
-            if q == 0:
-                quantise_z(0, 2)
-                y_pass(2, 0)
-                y_pass(3, 0)
-            if q < 3:
-                interleave(1, q, z_t1[q][:])
-        weigh_and_interleave1(3)
-        for q in (2, 3):
-            quantise_z(1, q)
-            y_pass(q, 1)
-        for q in range(4):
-            for n in range(2):
-                if (q, n) != (0, 0):
-                    sigmoid(q, n)
-                turn(q, n)
-        for q in range(4):
-            for n in range(2):
-                product(q, n)
-                if 2 * q + n < ON_GPSIMD:
-                    finish(nc.gpsimd, q, n)
-        for i in range(ON_GPSIMD, 8):
-            finish(nc.vector, i // 2, i % 2)
+        interleave(1, 0, z_t1[0][:])
+        for t in range(4):
+            weigh1(1, t)
+        interleave(1, 1, z_t1[1][:])
+
+        for t in range(4):
+            gather_b1(2, t, over="z_words00")
+        quantise_z(1, 0)
+        y_pass(0, 1)
+        gate(0)
+        for t in range(4):
+            gather_d1(2, t, over="z_words10")
+        quantise_z(1, 1)
+        y_pass(1, 1)
+        for t in range(4):
+            weigh1(2, t)
+        interleave(1, 2, z_t1[2][:])
+        interleave(0, 2, z_t0[1][:])
+        gate(1)
+        for t in range(4):
+            gather_b1(3, t, over="z_words11")
+        for t in range(4):
+            gather_d1(3, t)
+        for t in range(4):
+            weigh1(3, t)
+        interleave(1, 3, z_t1[3][:])
+        quantise_z(1, 2)
+        quantise_z(0, 2)
+        y_pass(2, 0)
+        y_pass(2, 1)
+        y_pass(3, 0)
+        gate(2)
+
+        finish_chunk(0)
+        quantise_z(1, 3)
+        y_pass(3, 1)
+        gate(3)
+        for q in range(1, 4):
+            finish_chunk(q)

@@ -53,7 +53,7 @@ def tile_list_sensor_gated_interpolation_kernel(
         ends0 = sb([P, 5 * NP], F32, "ends0")
         diffs0 = sb([P, 8 * NP], F32, "diffs0")
         under = {(2, 1): ends0[:, NP : 3 * NP], (2, 3): ends0[:, 3 * NP : 5 * NP]}
-        under.update({(1, 2): diffs0[:, 4 * NP : 8 * NP]})
+        under.update({(0, 3): diffs0[:, 2 * NP : 4 * NP], (1, 3): diffs0[:, 4 * NP : 6 * NP]})
         z_raw = sb([P, 4 * NP], BF16, "z_raw")
         gn0 = sb([P, 2, 2], F32, "gn0")
         gn1 = sb([P, 4], F32, "gn1")
@@ -87,7 +87,8 @@ def tile_list_sensor_gated_interpolation_kernel(
         nc.sync.dma_start(gn1[:], gain[BANK:H].rearrange("(p t) -> p t", t=4))
         load_w1(0, 2)
         load_w1(0, 3)
-        load_w1(1, 2, BANK)
+        load_w1(1, 2)
+        load_w1(1, 3)
         load_w1(2, 2)
         load_w1(2, 3)
         nc.sync.dma_start(w4_w[:].bitcast(I32), w4_words.rearrange("a p c -> p a c").bitcast(I32))
@@ -115,10 +116,7 @@ def tile_list_sensor_gated_interpolation_kernel(
             copy(sorted_w[a, c][:, :, p0:p1, :].rearrange("p u (m i) j -> p m j i u", i=2), src)
 
         def cast1(copy, a, c, t0=0, t1=4):
-            if (a, c) == (0, 2):
-                flat = diffs0[:, 2 * NP : 4 * NP].bitcast(BF16)
-                sorted_w[a, 2] = flat.rearrange("p (t m j) -> p t m j", t=4, j=4)
-            elif (a, 2) not in sorted_w:
+            if (a, 2) not in sorted_w:
                 sorted_w[a, 2] = sb([P, 4, P, 4], BF16, f"sorted_w{a}2")
             src = raw[a, c].rearrange("p j (m t) -> p m j t", t=4)[:, :, :, t0:t1]
             m0 = MID * (c - 2)
@@ -249,7 +247,7 @@ def tile_list_sensor_gated_interpolation_kernel(
 
         def product(q, n):
             d = diff1[q] if n else diff0[:, :, P * q : P * (q + 1)]
-            gated[q, n] = sb([P, 4, P], F32, f"gated{q}{n}", ("raw00", "raw01", "raw10", "raw11", "raw20", "raw02", "sorted_w00", "raw22")[2 * q + n])
+            gated[q, n] = sb([P, 4, P], F32, f"gated{q}{n}", ("raw00", "raw01", "raw10", "raw11", "raw20", "raw02", "sorted_w00", "raw12")[2 * q + n])
             nc.vector.tensor_tensor(gated[q, n][:], gate_ps[q, n][:].rearrange("p (t j) -> p t j", t=4), d, ALU.mult)
 
         def finish(engine, q, n):
@@ -296,7 +294,7 @@ def tile_list_sensor_gated_interpolation_kernel(
         quantise_w1(1, 1, 0, 2)
         gather_d0(0)
         cast1(nc.scalar.copy, 0, 2)
-        cast1(nc.vector.tensor_copy, 0, 3)
+        cast1(nc.scalar.copy, 0, 3)
         quantise_w1(2, 1, 0, 2)
         states(1, (0, 1))
         weigh0(0)
@@ -306,12 +304,12 @@ def tile_list_sensor_gated_interpolation_kernel(
         weigh0(1)
         move_z0(0, 0)
         move_z0(0, 1)
-        copy_out(0, 2, nc.scalar.copy, "raw02")
-        copy_out(0, 3, nc.scalar.copy, "raw03")
-        cast1(nc.scalar.copy, 1, 2, 0, 2)
+        cast1(nc.scalar.copy, 1, 2)
+        copy_out(0, 2, nc.scalar.copy, "raw12")
+        cast1(nc.scalar.copy, 1, 3)
         cast1(nc.scalar.copy, 2, 2)
+        copy_out(0, 3, nc.scalar.copy, "raw22")
         cast1(nc.scalar.copy, 2, 3)
-        cast1(nc.vector.tensor_copy, 1, 2, 2, 4)
         gather_b(0, 2)
         quantise_w1(1, 2, 0, 4)
         gather_d0(2)

@@ -20,8 +20,10 @@ ALU = mybir.AluOpType
 P = 128
 BANK = 512
 PASSES = K // BANK
-MID = P // 2
 QUARTER = 256
+MID = P // 2
+RUN = 2 * P
+HALF1 = 2
 
 
 def tile_list_sensor_gated_interpolation_kernel(
@@ -39,6 +41,9 @@ def tile_list_sensor_gated_interpolation_kernel(
         def bank(i, name):
             return psum.tile([P, BANK], F32, name=name, tag=f"bank{i}")
 
+        def listed(list_sb, first, count):
+            return list_sb[:, first // 16 : (first + count) // 16]
+
         offs_sb = lists.tile([P, S // 16], U16, name="offs_sb")
         pos1_sb = lists.tile([P, NP // 16], U16, name="pos1_sb")
         pos2_sb = lists.tile([P, NP // 16], U16, name="pos2_sb")
@@ -49,32 +54,35 @@ def tile_list_sensor_gated_interpolation_kernel(
         nc.gpsimd.memset(w4_sc[:], 0)
 
         tab_w = [sb([P, T], I32, f"tab_w{a}") for a in range(PASSES)]
-        raw = {}
-        ends0 = sb([P, 5 * NP], F32, "ends0")
-        diffs0 = sb([P, 8 * NP], F32, "diffs0")
-        under = {(2, 1): ends0[:, NP : 3 * NP], (2, 3): ends0[:, 3 * NP : 5 * NP]}
-        under.update({(0, 3): diffs0[:, 2 * NP : 4 * NP], (1, 3): diffs0[:, 4 * NP : 6 * NP]})
-        z_raw = sb([P, 4 * NP], BF16, "z_raw")
-        gn0 = sb([P, 2, 2], F32, "gn0")
-        gn1 = sb([P, 4], F32, "gn1")
+        b_room = sb([P, 4 * NP], F32, "b_room")
+        d_room = sb([P, 8 * NP], F32, "d_room")
+        z_room = sb([P, 4 * NP], BF16, "z_room")
+        end_b0 = b_room[:].rearrange("p (t j) -> p t j", t=4)
+        diff0 = d_room[:].rearrange("p (t j) -> p t j", t=4)[:, :, 0:NP]
+        weighed0 = z_room[:].rearrange("p (t j) -> p t j", t=4)
+        raw = {
+            (2, 1): b_room[:, NP : 3 * NP],
+            (0, 3): d_room[:, 2 * NP : 4 * NP],
+            (1, 3): d_room[:, 4 * NP : 6 * NP],
+        }
+        gain0 = sb([P, 2, 2], F32, "gain0")
+        gain1 = sb([P, 4], F32, "gain1")
         w4_w = sb([P, 2, 2 * H], U8, "w4_w")
 
         def load_table(a):
             nc.sync.dma_start(tab_w[a][:], tab_words[a].rearrange("p t i -> p (t i)").bitcast(I32))
 
-        def load_w1(a, c, width=QUARTER):
-            if (a, c) in under:
-                raw[a, c] = under[a, c].rearrange("p (j c) -> p j c", j=4)
-            else:
-                raw[a, c] = sb([P, 4, width], F32, f"raw{a}{c}")[:]
-            src = w1[BANK * a : BANK * (a + 1), QUARTER * c : QUARTER * c + width]
-            nc.sync.dma_start(raw[a, c], src.rearrange("(p j) c -> p j c", j=4))
+        def load_w1(a, c):
+            if (a, c) not in raw:
+                raw[a, c] = sb([P, 4 * QUARTER], F32, f"raw{a}{c}")[:]
+            src = w1[BANK * a : BANK * (a + 1), QUARTER * c : QUARTER * (c + 1)]
+            nc.sync.dma_start(raw[a, c].rearrange("p (j c) -> p j c", j=4), src.rearrange("(p j) c -> p j c", j=4))
 
         load_table(0)
         nc.sync.dma_start(offs_sb[:], offs)
         load_w1(0, 0)
-        for q in range(4):
-            nc.sync.dma_start(tab_sc[32 * q : 32 * q + 12, :], tab_scales[:, 4 * q : 4 * q + 4, :].bitcast(I32))
+        for g in range(4):
+            nc.sync.dma_start(tab_sc[32 * g : 32 * g + 12, :], tab_scales[:, 4 * g : 4 * g + 4, :].bitcast(I32))
         load_table(1)
         load_w1(1, 0)
         load_table(2)
@@ -83,59 +91,59 @@ def tile_list_sensor_gated_interpolation_kernel(
         nc.sync.dma_start(pos1_sb[:], pos1)
         for a in range(PASSES):
             load_w1(a, 1)
-        nc.sync.dma_start(gn0[:], gain[0:BANK].rearrange("(c p u) -> p c u", c=2, u=2))
-        nc.sync.dma_start(gn1[:], gain[BANK:H].rearrange("(p t) -> p t", t=4))
-        load_w1(0, 2)
-        load_w1(0, 3)
-        load_w1(1, 2)
-        load_w1(1, 3)
-        load_w1(2, 2)
-        load_w1(2, 3)
+        nc.sync.dma_start(gain0[:], gain[0:BANK].rearrange("(c p u) -> p c u", c=2, u=2))
+        nc.sync.dma_start(gain1[:], gain[BANK:H].rearrange("(p t) -> p t", t=4))
+        for a in range(PASSES):
+            load_w1(a, 2)
+            load_w1(a, 3)
         nc.sync.dma_start(w4_w[:].bitcast(I32), w4_words.rearrange("a p c -> p a c").bitcast(I32))
-        for q in range(4):
+        for g in range(4):
             nc.sync.dma_start(
-                w4_sc[32 * q : 32 * q + 4, :, :],
-                w4_scales[:, 4 * q : 4 * q + 4, :].rearrange("a r n -> r a n").bitcast(I32),
+                w4_sc[32 * g : 32 * g + 4, :, :],
+                w4_scales[:, 4 * g : 4 * g + 4, :].rearrange("a r n -> r a n").bitcast(I32),
             )
         ident = sb([P, P], F32, "ident")
         make_identity(nc, ident[:])
 
         v_sc = sb([P, S], U8, "v_sc")
-        v_w, sorted_w, w_c, w_s, h_ps, h = {}, {}, {}, {}, {}, {}
+        v_w, w_c, w_s, h_ps, h = {}, {}, {}, {}, {}
+        sorted_w = {
+            (1, 1): d_room[:, 0:NP].bitcast(BF16).rearrange("p (u m j) -> p u m j", u=2, j=4),
+            (2, 1): z_room[:, 0 : 2 * NP].rearrange("p (u m j) -> p u m j", u=2, j=4),
+        }
 
-        def gather_table(a, over=None):
-            v_w[a] = sb([P, S], U32, f"v_w{a}", over)
+        def gather_table(a):
+            v_w[a] = sb([P, S], U32, f"v_w{a}")
             nc.vector.tensor_copy(v_w[a][:], tab_w[a][:].bitcast(U32).indirect(offs_sb[:]))
 
-        def cast0(copy, a, c, p0=0, p1=P, over=None):
-            if (a, c) == (2, 1):
-                sorted_w[a, c] = z_raw[:, 0 : 2 * NP].rearrange("p (u m j) -> p u m j", u=2, j=4)
-            elif (a, c) not in sorted_w:
-                sorted_w[a, c] = sb([P, 2, P, 4], BF16, f"sorted_w{a}{c}", over)
-            src = raw[a, c][:, :, 2 * p0 : 2 * p1].rearrange("p j (m i u) -> p m j i u", i=2, u=2)
-            copy(sorted_w[a, c][:, :, p0:p1, :].rearrange("p u (m i) j -> p m j i u", i=2), src)
+        def cast0(a, c, copy=nc.scalar.copy, over=None):
+            if (a, c) not in sorted_w:
+                sorted_w[a, c] = sb([P, 2, P, 4], BF16, f"sorted_w{a}{c}", over)[:]
+            src = raw[a, c].rearrange("p (j m i u) -> p m j i u", j=4, i=2, u=2)
+            copy(sorted_w[a, c].rearrange("p u (m i) j -> p m j i u", i=2), src)
 
-        def cast1(copy, a, c, t0=0, t1=4):
-            if (a, 2) not in sorted_w:
-                sorted_w[a, 2] = sb([P, 4, P, 4], BF16, f"sorted_w{a}2")
-            src = raw[a, c].rearrange("p j (m t) -> p m j t", t=4)[:, :, :, t0:t1]
-            m0 = MID * (c - 2)
-            copy(sorted_w[a, 2][:, t0:t1, m0 : m0 + src.shape[1], :].rearrange("p t m j -> p m j t"), src)
+        def cast1(a, c, copy=nc.scalar.copy, t0=0, t1=4):
+            if (a, HALF1) not in sorted_w:
+                sorted_w[a, HALF1] = sb([P, 4, P, 4], BF16, f"sorted_w{a}{HALF1}")[:]
+            m0 = MID * (c - HALF1)
+            src = raw[a, c].rearrange("p (j m t) -> p m j t", j=4, t=4)[:, :, :, t0:t1]
+            copy(sorted_w[a, HALF1][:, t0:t1, m0 : m0 + MID, :].rearrange("p t m j -> p m j t"), src)
 
-        def quantise_w1(a, c, t0, t1):
-            codes, scales = sb([P, P * (t1 - t0)], U32, f"w_c{a}{c}{t0}"), sb([P, P * (t1 - t0)], U8, f"w_s{a}{c}{t0}")
+        def quantise_w1(a, c, i0, i1):
+            n = P * (i1 - i0)
+            codes, scales = sb([P, n], U32, f"w_c{a}{c}{i0}"), sb([P, n], U8, f"w_s{a}{c}{i0}")
             nc.vector.quantize_mx(
                 out=codes[:].bitcast(FP8X4),
                 scales=scales[:],
-                in_=sorted_w[a, c][:, t0:t1, :, :].rearrange("p t m j -> p (t m j)"),
+                in_=sorted_w[a, c][:, i0:i1, :, :].rearrange("p t m j -> p (t m j)"),
             )
-            for t in range(t0, t1):
-                cols = slice(P * (t - t0), P * (t - t0 + 1))
-                w_c[a, c, t], w_s[a, c, t] = codes[:, cols], scales[:, cols]
+            for i in range(i0, i1):
+                cols = slice(P * (i - i0), P * (i - i0 + 1))
+                w_c[a, c, i], w_s[a, c, i] = codes[:, cols], scales[:, cols]
 
-        def states(c, tiles):
-            for i in tiles:
-                b, t = (1, i) if c == 2 else (0, 2 * c + i)
+        def states(c):
+            for i in range(4 if c == HALF1 else 2):
+                b, t = (1, i) if c == HALF1 else (0, 2 * c + i)
                 for a in range(PASSES):
                     for s in range(2):
                         if a == 0:
@@ -156,63 +164,54 @@ def tile_list_sensor_gated_interpolation_kernel(
             for s in range(2):
                 copy(h[b, t][:, BANK * s : BANK * (s + 1)], h_ps[b, t, s][:])
 
-        end_b0 = ends0[:, 0 : 4 * NP].rearrange("p (t j) -> p t j", t=4)
-        diff0 = diffs0[:].rearrange("p (t j) -> p t j", t=4)[:, :, 0:NP]
-        weighed0 = z_raw[:].rearrange("p (t j) -> p t j", t=4)
-        z_t0 = [sb([P, 4, 2 * P], BF16, f"z_t0_{i}") for i in range(2)]
-        end_b1 = {}
-        diff1, z_t1, z_words, z_c, z_s, y_ps, turned, gate_ps, gated = {}, {}, {}, {}, {}, {}, {}, {}, {}
+        z_t0 = [sb([P, 4, RUN], BF16, f"z_t0_{i}") for i in range(2)]
+        end_b1, diff1, z_t1, z_words, z_c, z_s, y_ps, gate_ps = {}, {}, {}, {}, {}, {}, {}, {}
 
-        def gather_b(b, t):
-            nc.vector.tensor_copy(end_b0[:, t, :], h[b, t][:].indirect(pos2_sb[:, :]))
+        def gather_b0(t):
+            nc.vector.tensor_copy(end_b0[:, t, :], h[0, t][:].indirect(pos2_sb[:, :]))
+
+        def gather_d0(t, first=0, count=NP):
+            pairs = slice(first, first + count)
+            picked = h[0, t][:].indirect(listed(pos1_sb, first, count))
+            nc.vector.tensor_tensor(diff0[:, t, pairs], picked, end_b0[:, t, pairs], ALU.subtract)
+
+        def weigh0(t, first=0, count=NP):
+            pairs = slice(first, first + count)
+            factor = gain0[:, t // 2, t % 2 : t % 2 + 1]
+            nc.gpsimd.tensor_scalar(weighed0[:, t, pairs], diff0[:, t, pairs], factor, 0.0, ALU.mult, ALU.add)
+
+        def move_z0(c, i):
+            for e in range(2):
+                src = weighed0[e:P:2, 2 * c : 2 * c + 2, RUN * i : RUN * (i + 1)]
+                nc.sync.dma_start(z_t0[i][MID * c : MID * (c + 1), 2 * e : 2 * e + 2, :], src)
 
         def gather_b1(q, t, over=None):
             if q not in end_b1:
                 end_b1[q] = sb([P, 4, P], F32, f"end_b1_{q}", over)[:]
-            nc.vector.tensor_copy(end_b1[q][:, t, :], h[1, t][:].indirect(pos2_sb[:, 8 * q : 8 * (q + 1)]))
+            nc.vector.tensor_copy(end_b1[q][:, t, :], h[1, t][:].indirect(listed(pos2_sb, P * q, P)))
 
-        def gather_d0(t, i0=0, i1=2):
-            pairs = slice(2 * P * i0, 2 * P * i1)
-            picked = h[0, t][:].indirect(pos1_sb[:, 16 * i0 : 16 * i1])
-            nc.vector.tensor_tensor(diff0[:, t, pairs], picked, end_b0[:, t, pairs], ALU.subtract)
-
-        def weigh0(t, i0=0, i1=2):
-            pairs = slice(2 * P * i0, 2 * P * i1)
-            d = diff0[:, t, pairs]
-            factor = gn0[:, t // 2, t % 2 : t % 2 + 1]
-            nc.gpsimd.tensor_scalar(weighed0[:, t, pairs], d, factor, 0.0, ALU.mult, ALU.add)
-
-        def move_z0(c, i):
-            pairs = slice(2 * P * i, 2 * P * (i + 1))
-            for e in range(2):
-                src = weighed0[e:P:2, 2 * c : 2 * c + 2, pairs]
-                nc.sync.dma_start(z_t0[i][MID * c : MID * (c + 1), 2 * e : 2 * e + 2, :], src)
-
-        def gather_d1(q, t, over=None):
+        def gather_d1(q, t):
             if q not in diff1:
-                diff1[q] = sb([P, 4, P], F32, f"diff1_{q}", over)[:]
-            picked = h[1, t][:].indirect(pos1_sb[:, 8 * q : 8 * (q + 1)])
+                diff1[q] = sb([P, 4, P], F32, f"diff1_{q}")[:]
+            picked = h[1, t][:].indirect(listed(pos1_sb, P * q, P))
             nc.vector.tensor_tensor(diff1[q][:, t, :], picked, end_b1[q][:, t, :], ALU.subtract)
 
         def weigh1(q, t):
-            if q == 0 and t == 0:
-                both = sb([P, 2, 4, P], BF16, "z_t1_01", "z_raw")
-                z_t1[0], z_t1[1] = both[:, 0, :, :], both[:, 1, :, :]
-            elif q not in z_t1:
-                z_t1[q] = sb([P, 4, P], BF16, f"z_t1_{q}")
-            nc.scalar.activation(z_t1[q][:, t, :], diff1[q][:, t, :], ACT.Copy, scale=gn1[:, t : t + 1])
+            if q not in z_t1:
+                z_t1[q] = sb([P, 4, P], BF16, f"z_t1_{q}")[:]
+            nc.scalar.activation(z_t1[q][:, t, :], diff1[q][:, t, :], ACT.Copy, scale=gain1[:, t : t + 1])
 
         def interleave(b, q, src):
             z_words[b, q] = sb([P, src.shape[2], 4], BF16, f"z_words{b}{q}")
             nc.scalar.copy(
-                z_words[b, q][:].rearrange("p (c i) t -> p c t i", i=4), src.rearrange("p t (c i) -> p c t i", i=4)
+                z_words[b, q][:].rearrange("p (x i) j -> p x j i", i=4), src.rearrange("p j (x i) -> p x j i", i=4)
             )
 
         def quantise_z(b, q):
             n = z_words[b, q].shape[1]
             codes, scales = sb([P, n], U32, f"z_c{b}{q}"), sb([P, n], U8, f"z_s{b}{q}")
             nc.vector.quantize_mx(
-                out=codes[:].bitcast(FP8X4), scales=scales[:], in_=z_words[b, q][:].rearrange("p j t -> p (j t)")
+                out=codes[:].bitcast(FP8X4), scales=scales[:], in_=z_words[b, q][:].rearrange("p x j -> p (x j)")
             )
             for i in range(n // P):
                 z_c[b, q + i], z_s[b, q + i] = codes[:, P * i : P * (i + 1)], scales[:, P * i : P * (i + 1)]
@@ -231,101 +230,96 @@ def tile_list_sensor_gated_interpolation_kernel(
                     stop=(b == 1),
                 )
 
-        def sigmoid(q, n):
-            turned[q, n] = sb([P, 4, P], F32, f"turned{q}{n}")
-            if n == 0:
-                dst = turned[q, n][:].rearrange("p (c u) m -> p c u m", c=2)
-                src = y_ps[q, n][:].rearrange("p (c m u) -> p c u m", c=2, u=2)
-            else:
-                dst, src = turned[q, n][:], y_ps[q, n][:].rearrange("p (m t) -> p t m", t=4)
-            nc.scalar.activation(dst, src, ACT.Sigmoid)
-
-        def turn(q, n):
-            gate_ps[q, n] = bank(2 * q + n, f"gate_ps{q}{n}")
-            for t in range(4):
-                nc.tensor.transpose(gate_ps[q, n][:, P * t : P * (t + 1)], turned[q, n][:, t, :], ident[:])
-
-        def product(q, n):
-            d = diff1[q] if n else diff0[:, :, P * q : P * (q + 1)]
-            gated[q, n] = sb([P, 4, P], F32, f"gated{q}{n}", ("raw00", "raw01", "raw10", "raw11", "raw20", "raw02", "sorted_w00", "raw12")[2 * q + n])
-            nc.vector.tensor_tensor(gated[q, n][:], gate_ps[q, n][:].rearrange("p (t j) -> p t j", t=4), d, ALU.mult)
-
-        def finish(engine, q, n):
-            pairs = slice(P * q, P * (q + 1))
-            res = sb([P, 4, P], F32, f"res{q}{n}")
-            engine.tensor_tensor(res[:], gated[q, n][:], end_b1[q] if n else end_b0[:, :, pairs], ALU.add)
-            if n:
-                nc.sync.dma_start(out[BANK:H, pairs].rearrange("(p t) j -> p t j", t=4), res[:])
-            else:
-                for c in range(2):
-                    rows = out[QUARTER * c : QUARTER * (c + 1), pairs]
-                    nc.sync.dma_start(rows.rearrange("(p u) j -> p u j", u=2), res[:, 2 * c : 2 * c + 2, :])
-
         def gate(q):
             for n in range(2):
-                sigmoid(q, n)
-                turn(q, n)
+                turned = sb([P, 4, P], F32, f"turned{q}{n}")
+                if n == 0:
+                    dst = turned[:].rearrange("p (c u) m -> p c u m", c=2)
+                    src = y_ps[q, n][:].rearrange("p (c m u) -> p c u m", c=2, u=2)
+                else:
+                    dst, src = turned[:], y_ps[q, n][:].rearrange("p (m t) -> p t m", t=4)
+                nc.scalar.activation(dst, src, ACT.Sigmoid)
+                gate_ps[q, n] = bank(2 * q + n, f"gate_ps{q}{n}")
+                for t in range(4):
+                    nc.tensor.transpose(gate_ps[q, n][:, P * t : P * (t + 1)], turned[:, t, :], ident[:])
 
-        def finish_chunk(q):
-            for n in range(2):
-                product(q, n)
-            for n in range(2):
-                finish(nc.vector, q, n)
+        def finish(q):
+            pairs = slice(P * q, P * (q + 1))
+            gated = [sb([P, 4, P], F32, f"gated{q}{n}") for n in range(2)]
+            res = [sb([P, 4, P], F32, f"res{q}{n}") for n in range(2)]
+            for n, d in enumerate((diff0[:, :, pairs], diff1[q])):
+                nc.vector.tensor_tensor(gated[n][:], gate_ps[q, n][:].rearrange("p (t x) -> p t x", t=4), d, ALU.mult)
+            nc.vector.tensor_tensor(res[0][:], gated[0][:], end_b0[:, :, pairs], ALU.add)
+            for c in range(2):
+                rows = out[QUARTER * c : QUARTER * (c + 1), pairs]
+                nc.sync.dma_start(rows.rearrange("(p u) x -> p u x", u=2), res[0][:, 2 * c : 2 * c + 2, :])
+            nc.vector.tensor_tensor(res[1][:], gated[1][:], end_b1[q], ALU.add)
+            nc.sync.dma_start(out[BANK:H, pairs].rearrange("(p t) x -> p t x", t=4), res[1][:])
 
         gather_table(0)
         nc.vector.tensor_copy(v_sc[:], tab_sc[:].bitcast(U8).indirect(offs_sb[:]))
-        cast0(nc.scalar.copy, 0, 0)
+        cast0(0, 0)
         quantise_w1(0, 0, 0, 2)
         gather_table(1)
-        cast0(nc.scalar.copy, 1, 0)
+        cast0(1, 0)
         quantise_w1(1, 0, 0, 2)
         gather_table(2)
-        cast0(nc.scalar.copy, 2, 0)
+        cast0(2, 0)
         quantise_w1(2, 0, 0, 1)
         quantise_w1(2, 0, 1, 2)
-        states(0, (0, 1))
-        cast0(nc.vector.tensor_copy, 0, 1, over="raw20")
+        states(0)
+
+        cast0(0, 1, nc.vector.tensor_copy, "raw20")
         quantise_w1(0, 1, 0, 2)
         copy_out(0, 0, nc.vector.tensor_copy)
-        cast0(nc.scalar.copy, 1, 1)
+        cast0(1, 1)
         copy_out(0, 1, nc.scalar.copy, "raw11")
-        cast0(nc.scalar.copy, 2, 1)
-        gather_b(0, 0)
+        cast0(2, 1)
+        gather_b0(0)
         quantise_w1(1, 1, 0, 2)
         gather_d0(0)
-        cast1(nc.scalar.copy, 0, 2)
-        cast1(nc.scalar.copy, 0, 3)
+        cast1(0, 2)
+        cast1(0, 3)
         quantise_w1(2, 1, 0, 2)
-        states(1, (0, 1))
+        states(1)
         weigh0(0)
-        gather_b(0, 1)
-        quantise_w1(0, 2, 0, 4)
+
+        gather_b0(1)
+        quantise_w1(0, HALF1, 0, 4)
         gather_d0(1)
         weigh0(1)
-        move_z0(0, 0)
-        move_z0(0, 1)
-        cast1(nc.scalar.copy, 1, 2)
+        for i in range(2):
+            move_z0(0, i)
+        cast1(1, 2)
         copy_out(0, 2, nc.scalar.copy, "raw12")
-        cast1(nc.scalar.copy, 1, 3)
-        cast1(nc.scalar.copy, 2, 2)
+        cast1(1, 3)
+
+        gather_b0(2)
+        cast1(2, 3, nc.vector.tensor_copy, 0, 2)
+        cast1(2, 2)
         copy_out(0, 3, nc.scalar.copy, "raw22")
-        cast1(nc.scalar.copy, 2, 3)
-        gather_b(0, 2)
-        quantise_w1(1, 2, 0, 4)
+        cast1(2, 3, nc.scalar.copy, 2, 4)
+        quantise_w1(1, HALF1, 0, 4)
         gather_d0(2)
         weigh0(2)
-        quantise_w1(2, 2, 0, 1)
-        gather_b(0, 3)
-        quantise_w1(2, 2, 1, 2)
-        quantise_w1(2, 2, 2, 4)
-        states(2, range(4))
+
+        quantise_w1(2, HALF1, 0, 1)
+        gather_b0(3)
+        quantise_w1(2, HALF1, 1, 2)
+        quantise_w1(2, HALF1, 2, 4)
+        states(HALF1)
         for i in range(2):
-            gather_d0(3, i, i + 1)
-            weigh0(3, i, i + 1)
+            gather_d0(3, RUN * i, RUN)
+            weigh0(3, RUN * i, RUN)
             move_z0(1, i)
+
         for t, over in enumerate(("tab_w0", "tab_w1", "tab_w2", "h00")):
             copy_out(1, t, nc.scalar.copy, over)
         interleave(0, 0, z_t0[0][:])
+
+        later = sb([P, 2 * BANK], F32, "later", "z_room")[:].rearrange("p (i t x) -> p i t x", i=2, t=4)
+        diff1[2], end_b1[3] = later[:, 0, :, :], later[:, 1, :, :]
+        z_t1[0], z_t1[1] = diff1[2].bitcast(BF16)[:, :, 0:P], end_b1[3].bitcast(BF16)[:, :, 0:P]
 
         for t in range(4):
             gather_b1(0, t)
@@ -336,32 +330,32 @@ def tile_list_sensor_gated_interpolation_kernel(
         quantise_z(0, 0)
         y_pass(0, 0)
         y_pass(1, 0)
-        interleave(1, 0, z_t1[0][:])
+        interleave(1, 0, z_t1[0])
         for t in range(4):
             weigh1(1, t)
-        interleave(1, 1, z_t1[1][:])
+        interleave(1, 1, z_t1[1])
 
         for t in range(4):
-            gather_b1(2, t, over="z_words00")
+            gather_b1(2, t, over="z_t0_0")
         quantise_z(1, 0)
         y_pass(0, 1)
         gate(0)
         for t in range(4):
-            gather_d1(2, t, over="z_words10")
+            gather_d1(2, t)
         quantise_z(1, 1)
         y_pass(1, 1)
         for t in range(4):
             weigh1(2, t)
-        interleave(1, 2, z_t1[2][:])
+        interleave(1, 2, z_t1[2])
         interleave(0, 2, z_t0[1][:])
         gate(1)
         for t in range(4):
-            gather_b1(3, t, over="z_words11")
+            gather_b1(3, t)
         for t in range(4):
             gather_d1(3, t)
         for t in range(4):
             weigh1(3, t)
-        interleave(1, 3, z_t1[3][:])
+        interleave(1, 3, z_t1[3])
         quantise_z(1, 2)
         quantise_z(0, 2)
         y_pass(2, 0)
@@ -369,9 +363,9 @@ def tile_list_sensor_gated_interpolation_kernel(
         y_pass(3, 0)
         gate(2)
 
-        finish_chunk(0)
+        finish(0)
         quantise_z(1, 3)
         y_pass(3, 1)
         gate(3)
         for q in range(1, 4):
-            finish_chunk(q)
+            finish(q)

@@ -23,6 +23,7 @@ PASSES = K // BANK
 QUARTER = 256
 MID = P // 2
 RUN = 2 * P
+SUMMED = (0, 1, 2)
 HALF1 = 2
 
 
@@ -65,7 +66,7 @@ def tile_list_sensor_gated_interpolation_kernel(
             (0, 3): d_room[:, 2 * NP : 4 * NP],
             (1, 3): d_room[:, 4 * NP : 6 * NP],
         }
-        gain0 = sb([P, 2, 2], F32, "gain0")
+        gain0 = sb([P, 4], F32, "gain0")
         gain1 = sb([P, 4], F32, "gain1")
         w4_w = sb([P, 2, 2 * H], U8, "w4_w")
 
@@ -91,7 +92,8 @@ def tile_list_sensor_gated_interpolation_kernel(
         nc.sync.dma_start(pos1_sb[:], pos1)
         for a in range(PASSES):
             load_w1(a, 1)
-        nc.sync.dma_start(gain0[:], gain[0:BANK].rearrange("(c p u) -> p c u", c=2, u=2))
+        with nc.allow_non_contiguous_dma(reason="one factor a partition and tile"):
+            nc.sync.dma_start(gain0[:], gain[0:BANK].rearrange("(t p) -> p t", t=4))
         nc.sync.dma_start(gain1[:], gain[BANK:H].rearrange("(p t) -> p t", t=4))
         for a in range(PASSES):
             load_w1(a, 2)
@@ -119,8 +121,8 @@ def tile_list_sensor_gated_interpolation_kernel(
         def cast0(a, c, copy=nc.scalar.copy, over=None):
             if (a, c) not in sorted_w:
                 sorted_w[a, c] = sb([P, 2, P, 4], BF16, f"sorted_w{a}{c}", over)[:]
-            src = raw[a, c].rearrange("p (j m i u) -> p m j i u", j=4, i=2, u=2)
-            copy(sorted_w[a, c].rearrange("p u (m i) j -> p m j i u", i=2), src)
+            src = raw[a, c].rearrange("p (j x i) -> p x j i", j=4, i=4)
+            copy(sorted_w[a, c].rearrange("p u (x i) j -> p (u x) j i", i=4), src)
 
         def cast1(a, c, copy=nc.scalar.copy, t0=0, t1=4):
             if (a, HALF1) not in sorted_w:
@@ -164,8 +166,13 @@ def tile_list_sensor_gated_interpolation_kernel(
             for s in range(2):
                 copy(h[b, t][:, BANK * s : BANK * (s + 1)], h_ps[b, t, s][:])
 
-        z_t0 = [sb([P, 4, RUN], BF16, f"z_t0_{i}") for i in range(2)]
-        end_b1, diff1, z_t1, z_words, z_c, z_s, y_ps, gate_ps = {}, {}, {}, {}, {}, {}, {}, {}
+        d_run = sb([P, 5 * RUN], F32, "d_run")
+        z_t0 = [
+            d_run[:, 3 * RUN : 5 * RUN].bitcast(BF16).rearrange("p (j x) -> p j x", j=4),
+            sb([P, 4, RUN], BF16, "z_t0_1")[:],
+        ]
+        end_b1, diff1, z_t1, z_words, z_c, z_s, y_ps = {}, {}, {}, {}, {}, {}, {}
+        factors, turned, b_turned, gated, res = {}, {}, {}, {}, {}
 
         def gather_b0(t):
             nc.vector.tensor_copy(end_b0[:, t, :], h[0, t][:].indirect(pos2_sb[:, :]))
@@ -177,13 +184,12 @@ def tile_list_sensor_gated_interpolation_kernel(
 
         def weigh0(t, first=0, count=NP):
             pairs = slice(first, first + count)
-            factor = gain0[:, t // 2, t % 2 : t % 2 + 1]
+            factor = gain0[:, t : t + 1]
             nc.gpsimd.tensor_scalar(weighed0[:, t, pairs], diff0[:, t, pairs], factor, 0.0, ALU.mult, ALU.add)
 
         def move_z0(c, i):
-            for e in range(2):
-                src = weighed0[e:P:2, 2 * c : 2 * c + 2, RUN * i : RUN * (i + 1)]
-                nc.sync.dma_start(z_t0[i][MID * c : MID * (c + 1), 2 * e : 2 * e + 2, :], src)
+            for t in (2 * c, 2 * c + 1):
+                nc.sync.dma_start(z_t0[i][32 * t : 32 * (t + 1), :, :], weighed0[:, t, RUN * i : RUN * (i + 1)])
 
         def gather_b1(q, t, over=None):
             if q not in end_b1:
@@ -201,6 +207,11 @@ def tile_list_sensor_gated_interpolation_kernel(
                 z_t1[q] = sb([P, 4, P], BF16, f"z_t1_{q}")[:]
             nc.scalar.activation(z_t1[q][:, t, :], diff1[q][:, t, :], ACT.Copy, scale=gain1[:, t : t + 1])
 
+        def weigh_words(q):
+            z_words[1, q] = sb([P, P, 4], BF16, f"z_words1{q}")
+            factor = gain1[:].unsqueeze(1).to_broadcast([P, P, 4])
+            nc.gpsimd.tensor_tensor(z_words[1, q][:], diff1[q].rearrange("p t x -> p x t"), factor, ALU.mult)
+
         def interleave(b, q, src):
             z_words[b, q] = sb([P, src.shape[2], 4], BF16, f"z_words{b}{q}")
             nc.scalar.copy(
@@ -217,44 +228,82 @@ def tile_list_sensor_gated_interpolation_kernel(
                 z_c[b, q + i], z_s[b, q + i] = codes[:, P * i : P * (i + 1)], scales[:, P * i : P * (i + 1)]
 
         def y_pass(q, b):
-            for n in range(2):
-                if b == 0:
+            if b == 0:
+                for n in range(2):
                     y_ps[q, n] = bank(2 * q + n, f"y_ps{q}{n}")
+            nc.tensor.matmul_mx(
+                out=y_ps[q, 1][:],
+                lhsT=z_c[b, q].bitcast(FP8X4),
+                lhsT_scale=z_s[b, q],
+                rhs=w4_w[:, b, 2 * BANK : 4 * BANK].bitcast(FP4X4),
+                rhs_scale=w4_sc[:, b, P : 2 * P].bitcast(U8),
+                start=(b == 0),
+                stop=(b == 1),
+            )
+            for t in range(4):
                 nc.tensor.matmul_mx(
-                    out=y_ps[q, n][:],
-                    lhsT=z_c[b, q].bitcast(FP8X4),
-                    lhsT_scale=z_s[b, q],
-                    rhs=w4_w[:, b, 2 * BANK * n : 2 * BANK * (n + 1)].bitcast(FP4X4),
-                    rhs_scale=w4_sc[:, b, P * n : P * (n + 1)].bitcast(U8),
-                    start=(b == 0),
-                    stop=(b == 1),
+                    out=y_ps[q, 0][:, P * t : P * (t + 1)],
+                    lhsT=w4_w[:, b, 2 * P * t : 2 * P * (t + 1)].bitcast(FP4X4),
+                    lhsT_scale=w4_sc[:, b, 32 * t : 32 * (t + 1)].bitcast(U8),
+                    rhs=z_c[b, q].bitcast(FP8X4),
+                    rhs_scale=z_s[b, q],
+                    start=(b == 0 and t == 0),
+                    stop=(b == 1 and t == 3),
                 )
 
-        def gate(q):
-            for n in range(2):
-                turned = sb([P, 4, P], F32, f"turned{q}{n}")
-                if n == 0:
-                    dst = turned[:].rearrange("p (c u) m -> p c u m", c=2)
-                    src = y_ps[q, n][:].rearrange("p (c m u) -> p c u m", c=2, u=2)
-                else:
-                    dst, src = turned[:], y_ps[q, n][:].rearrange("p (m t) -> p t m", t=4)
-                nc.scalar.activation(dst, src, ACT.Sigmoid)
-                gate_ps[q, n] = bank(2 * q + n, f"gate_ps{q}{n}")
-                for t in range(4):
-                    nc.tensor.transpose(gate_ps[q, n][:, P * t : P * (t + 1)], turned[:, t, :], ident[:])
+        def by_tile(ps):
+            return ps[:].rearrange("p (t x) -> p t x", t=4)
 
-        def finish(q):
+        def turn(dst, src, first=True, last=True):
+            for t in range(4):
+                start, stop = (True, True) if first and last else (first and t == 0, last and t == 3)
+                nc.tensor.matmul(dst[:, P * t : P * (t + 1)], src[:, t, :], ident[:], start, stop, is_transpose=True)
+
+        def turn_b1(q, i, over=None):
+            b_ps = bank(i, f"b_ps{q}")
+            turn(b_ps, end_b1[q])
+            b_turned[q] = sb([P, 4, P], F32, f"b_turned{q}", over)
+            nc.scalar.activation(b_turned[q][:], by_tile(b_ps), ACT.Copy, scale=2.0)
+
+        def gate(q):
+            if q not in turned:
+                turned[q] = sb([P, 4, P], F32, f"turned{q}")[:]
+            nc.scalar.activation(turned[q], y_ps[q, 1][:].rearrange("p (m t) -> p t m", t=4), ACT.Tanh, scale=0.5)
+            other_ps = bank(2 * q + 1, f"other_ps{q}")
+            turn(other_ps, diff1[q] if q in SUMMED else turned[q])
+            gate0 = sb([P, 4, P], F32, f"gate0_{q}")
+            nc.scalar.activation(gate0[:], by_tile(y_ps[q, 0]), ACT.Tanh, scale=0.5)
+            factors[q, 0] = (gate0[:], diff0[:, :, P * q : P * (q + 1)])
+            factors[q, 1] = (turned[q], by_tile(other_ps)) if q in SUMMED else (by_tile(other_ps), diff1[q])
+
+        def store(q, n):
             pairs = slice(P * q, P * (q + 1))
-            gated = [sb([P, 4, P], F32, f"gated{q}{n}") for n in range(2)]
-            res = [sb([P, 4, P], F32, f"res{q}{n}") for n in range(2)]
-            for n, d in enumerate((diff0[:, :, pairs], diff1[q])):
-                nc.vector.tensor_tensor(gated[n][:], gate_ps[q, n][:].rearrange("p (t x) -> p t x", t=4), d, ALU.mult)
-            nc.vector.tensor_tensor(res[0][:], gated[0][:], end_b0[:, :, pairs], ALU.add)
-            for c in range(2):
-                rows = out[QUARTER * c : QUARTER * (c + 1), pairs]
-                nc.sync.dma_start(rows.rearrange("(p u) x -> p u x", u=2), res[0][:, 2 * c : 2 * c + 2, :])
-            nc.vector.tensor_tensor(res[1][:], gated[1][:], end_b1[q], ALU.add)
-            nc.sync.dma_start(out[BANK:H, pairs].rearrange("(p t) x -> p t x", t=4), res[1][:])
+            if n == 0:
+                rows = out[0:BANK, pairs].rearrange("(t p) x -> p t x", t=4)
+            else:
+                rows = out[BANK:H, pairs].rearrange("(p t) x -> p t x", t=4)
+            nc.sync.dma_start(rows, res[q, n])
+
+        def product(q, n):
+            if (q, n) not in gated:
+                gated[q, n] = sb([P, 4, P], F32, f"gated{q}{n}")[:]
+            tanh, d = factors[q, n]
+            nc.vector.scalar_tensor_tensor(gated[q, n], tanh, 1.0, d, ALU.add, ALU.mult)
+
+        def add(q, n):
+            res[q, n] = sb([P, 4, P], F32, f"res{q}{n}")[:]
+            b = end_b1[q] if n else end_b0[:, :, P * q : P * (q + 1)]
+            nc.vector.scalar_tensor_tensor(res[q, n], gated[q, n], 0.5, b, ALU.mult, ALU.add)
+            store(q, n)
+
+        def add_turned(q):
+            sum_ps = bank(2 * q, f"sum_ps{q}")
+            turn(sum_ps, b_turned[q], last=False)
+            turn(sum_ps, gated[q, 1], first=False)
+            if (q, 1) not in res:
+                res[q, 1] = sb([P, 4, P], F32, f"res{q}1")[:]
+            nc.scalar.activation(res[q, 1], by_tile(sum_ps), ACT.Copy, scale=0.5)
+            store(q, 1)
 
         gather_table(0)
         nc.vector.tensor_copy(v_sc[:], tab_sc[:].bitcast(U8).indirect(offs_sb[:]))
@@ -315,57 +364,74 @@ def tile_list_sensor_gated_interpolation_kernel(
 
         for t, over in enumerate(("tab_w0", "tab_w1", "tab_w2", "h00")):
             copy_out(1, t, nc.scalar.copy, over)
-        interleave(0, 0, z_t0[0][:])
+        interleave(0, 0, z_t0[0])
+        interleave(0, 2, z_t0[1])
 
-        later = sb([P, 2 * BANK], F32, "later", "z_room")[:].rearrange("p (i t x) -> p i t x", i=2, t=4)
-        diff1[2], end_b1[3] = later[:, 0, :, :], later[:, 1, :, :]
-        z_t1[0], z_t1[1] = diff1[2].bitcast(BF16)[:, :, 0:P], end_b1[3].bitcast(BF16)[:, :, 0:P]
+        diff1[2] = sb([P, 4, P], F32, "diff1_2", "z_room")[:]
+        z_t1[0] = diff1[2].bitcast(BF16)[:, :, 0:P]
+
+        for q in range(2):
+            diff1[q] = d_run[:, 0 : 4 * RUN].rearrange("p (t x) -> p t x", t=4)[:, :, P * q : P * (q + 1)]
+        room3 = sb([P, 4 * BANK], F32, "room3")[:]
+        z_t1[3] = room3.rearrange("p (t x) -> p t x", t=4).bitcast(BF16)[:, :, 0:P]
+        part3 = room3.rearrange("p (i t x) -> p i t x", i=4, t=4)
+        gated[1, 0], gated[1, 1], turned[2], res[0, 1] = (part3[:, i, :, :] for i in range(4))
 
         for t in range(4):
             gather_b1(0, t)
             gather_b1(1, t)
+            if t == 3:
+                quantise_z(0, 0)
             gather_d1(0, t)
             gather_d1(1, t)
+        weigh_words(1)
+        for t in range(4):
             weigh1(0, t)
-        quantise_z(0, 0)
+        quantise_z(0, 2)
         y_pass(0, 0)
         y_pass(1, 0)
+        turn_b1(0, 4, "z_words00")
         interleave(1, 0, z_t1[0])
+        turn_b1(1, 6, "z_words02")
         for t in range(4):
-            weigh1(1, t)
-        interleave(1, 1, z_t1[1])
-
-        for t in range(4):
-            gather_b1(2, t, over="z_t0_0")
+            gather_b1(2, t, over="z_t0_1")
+        turn_b1(2, 4)
         quantise_z(1, 0)
         y_pass(0, 1)
-        gate(0)
-        for t in range(4):
-            gather_d1(2, t)
         quantise_z(1, 1)
         y_pass(1, 1)
         for t in range(4):
-            weigh1(2, t)
-        interleave(1, 2, z_t1[2])
-        interleave(0, 2, z_t0[1][:])
-        gate(1)
+            gather_d1(2, t)
+        weigh_words(2)
+        y_pass(2, 0)
+        y_pass(3, 0)
+        gate(0)
         for t in range(4):
-            gather_b1(3, t)
+            gather_b1(3, t, over="z_words10")
         for t in range(4):
             gather_d1(3, t)
+        gate(1)
+        quantise_z(1, 2)
+        y_pass(2, 1)
         for t in range(4):
             weigh1(3, t)
         interleave(1, 3, z_t1[3])
-        quantise_z(1, 2)
-        quantise_z(0, 2)
-        y_pass(2, 0)
-        y_pass(2, 1)
-        y_pass(3, 0)
         gate(2)
 
-        finish(0)
+        part2 = sb([P, 2 * BANK], F32, "gated0", "z_words12")[:].rearrange("p (i t x) -> p i t x", i=2, t=4)
+        gated[0, 0], gated[0, 1] = part2[:, 0, :, :], part2[:, 1, :, :]
+        product(0, 1)
+        product(0, 0)
+        add(0, 0)
         quantise_z(1, 3)
         y_pass(3, 1)
         gate(3)
         for q in range(1, 4):
-            finish(q)
+            product(q, 1)
+            product(q, 0)
+            if q == 3:
+                add(q, 1)
+            add(q, 0)
+        add_turned(0)
+        add_turned(1)
+        add_turned(2)

from contextlib import ExitStack

import concourse.mybir as mybir
from concourse.masks import make_identity

K, T, S, NP, H = 1536, 2048, 1024, 512, 1024
FLOPS = 2 * K * H * S + 2 * H * H * NP

F32 = mybir.dt.float32
BF16 = mybir.dt.bfloat16
I32 = mybir.dt.int32
U32 = mybir.dt.uint32
U16 = mybir.dt.uint16
U8 = mybir.dt.uint8
FP8X4 = mybir.dt.float8_e4m3fn_x4
FP4X4 = mybir.dt.float4_e2m1fn_x4
ACT = mybir.ActivationFunctionType
ALU = mybir.AluOpType

P = 128
BANK = 512
PASSES = K // BANK
QUARTER = 256
MID = P // 2
RUN = 2 * P
SUMMED = (0, 1, 2)
HALF1 = 2


def tile_list_sensor_gated_interpolation_kernel(
    tc, tab_words, tab_scales, offs, w1, pos1, pos2, gain, w4_words, w4_scales, out
):
    nc = tc.nc
    with ExitStack() as ctx:
        lists = ctx.enter_context(tc.tile_pool(name="lists", bufs=1))
        keep = ctx.enter_context(tc.tile_pool(name="keep", bufs=1))
        psum = ctx.enter_context(tc.psum_pool(name="psum", bufs=1))

        def sb(shape, dtype, name, over=None):
            return keep.tile(shape, dtype, name=name, tag=over or name, align_bytes=64)

        def bank(i, name):
            return psum.tile([P, BANK], F32, name=name, tag=f"bank{i}")

        def listed(list_sb, first, count):
            return list_sb[:, first // 16 : (first + count) // 16]

        offs_sb = lists.tile([P, S // 16], U16, name="offs_sb")
        pos1_sb = lists.tile([P, NP // 16], U16, name="pos1_sb")
        pos2_sb = lists.tile([P, NP // 16], U16, name="pos2_sb")

        tab_sc = sb([P, T // 4], I32, "tab_sc")
        w4_sc = sb([P, 2, H // 4], I32, "w4_sc")
        nc.gpsimd.memset(tab_sc[:], 0)
        nc.gpsimd.memset(w4_sc[:], 0)

        tab_w = [sb([P, T], I32, f"tab_w{a}") for a in range(PASSES)]
        b_room = sb([P, 4 * NP], F32, "b_room")
        d_room = sb([P, 8 * NP], F32, "d_room")
        z_room = sb([P, 4 * NP], BF16, "z_room")
        end_b0 = b_room[:].rearrange("p (t j) -> p t j", t=4)
        diff0 = d_room[:].rearrange("p (t j) -> p t j", t=4)[:, :, 0:NP]
        weighed0 = z_room[:].rearrange("p (t j) -> p t j", t=4)
        raw = {
            (2, 1): b_room[:, NP : 3 * NP],
            (0, 3): d_room[:, 2 * NP : 4 * NP],
            (1, 3): d_room[:, 4 * NP : 6 * NP],
        }
        gain0 = sb([P, 4], F32, "gain0")
        gain1 = sb([P, 4], F32, "gain1")
        w4_w = sb([P, 2, 2 * H], U8, "w4_w")

        def load_table(a):
            nc.sync.dma_start(tab_w[a][:], tab_words[a].rearrange("p t i -> p (t i)").bitcast(I32))

        def load_w1(a, c):
            if (a, c) not in raw:
                raw[a, c] = sb([P, 4 * QUARTER], F32, f"raw{a}{c}")[:]
            src = w1[BANK * a : BANK * (a + 1), QUARTER * c : QUARTER * (c + 1)]
            nc.sync.dma_start(raw[a, c].rearrange("p (j c) -> p j c", j=4), src.rearrange("(p j) c -> p j c", j=4))

        load_table(0)
        nc.sync.dma_start(offs_sb[:], offs)
        load_w1(0, 0)
        for g in range(4):
            nc.sync.dma_start(tab_sc[32 * g : 32 * g + 12, :], tab_scales[:, 4 * g : 4 * g + 4, :].bitcast(I32))
        load_table(1)
        load_w1(1, 0)
        load_table(2)
        load_w1(2, 0)
        nc.sync.dma_start(pos2_sb[:], pos2)
        nc.sync.dma_start(pos1_sb[:], pos1)
        for a in range(PASSES):
            load_w1(a, 1)
        with nc.allow_non_contiguous_dma(reason="one factor a partition and tile"):
            nc.sync.dma_start(gain0[:], gain[0:BANK].rearrange("(t p) -> p t", t=4))
        nc.sync.dma_start(gain1[:], gain[BANK:H].rearrange("(p t) -> p t", t=4))
        for a in range(PASSES):
            load_w1(a, 2)
            load_w1(a, 3)
        nc.sync.dma_start(w4_w[:].bitcast(I32), w4_words.rearrange("a p c -> p a c").bitcast(I32))
        for g in range(4):
            nc.sync.dma_start(
                w4_sc[32 * g : 32 * g + 4, :, :],
                w4_scales[:, 4 * g : 4 * g + 4, :].rearrange("a r n -> r a n").bitcast(I32),
            )
        ident = sb([P, P], F32, "ident")
        make_identity(nc, ident[:])

        v_sc = sb([P, S], U8, "v_sc")
        v_w, w_c, w_s, h_ps, h = {}, {}, {}, {}, {}
        sorted_w = {
            (1, 1): d_room[:, 0:NP].bitcast(BF16).rearrange("p (u m j) -> p u m j", u=2, j=4),
            (2, 1): z_room[:, 0 : 2 * NP].rearrange("p (u m j) -> p u m j", u=2, j=4),
        }

        def gather_table(a):
            v_w[a] = sb([P, S], U32, f"v_w{a}")
            nc.vector.tensor_copy(v_w[a][:], tab_w[a][:].bitcast(U32).indirect(offs_sb[:]))

        def cast0(a, c, copy=nc.scalar.copy, over=None):
            if (a, c) not in sorted_w:
                sorted_w[a, c] = sb([P, 2, P, 4], BF16, f"sorted_w{a}{c}", over)[:]
            src = raw[a, c].rearrange("p (j x i) -> p x j i", j=4, i=4)
            copy(sorted_w[a, c].rearrange("p u (x i) j -> p (u x) j i", i=4), src)

        def cast1(a, c, copy=nc.scalar.copy, t0=0, t1=4):
            if (a, HALF1) not in sorted_w:
                sorted_w[a, HALF1] = sb([P, 4, P, 4], BF16, f"sorted_w{a}{HALF1}")[:]
            m0 = MID * (c - HALF1)
            src = raw[a, c].rearrange("p (j m t) -> p m j t", j=4, t=4)[:, :, :, t0:t1]
            copy(sorted_w[a, HALF1][:, t0:t1, m0 : m0 + MID, :].rearrange("p t m j -> p m j t"), src)

        def quantise_w1(a, c, i0, i1):
            n = P * (i1 - i0)
            codes, scales = sb([P, n], U32, f"w_c{a}{c}{i0}"), sb([P, n], U8, f"w_s{a}{c}{i0}")
            nc.vector.quantize_mx(
                out=codes[:].bitcast(FP8X4),
                scales=scales[:],
                in_=sorted_w[a, c][:, i0:i1, :, :].rearrange("p t m j -> p (t m j)"),
            )
            for i in range(i0, i1):
                cols = slice(P * (i - i0), P * (i - i0 + 1))
                w_c[a, c, i], w_s[a, c, i] = codes[:, cols], scales[:, cols]

        def states(c):
            for i in range(4 if c == HALF1 else 2):
                b, t = (1, i) if c == HALF1 else (0, 2 * c + i)
                for a in range(PASSES):
                    for s in range(2):
                        if a == 0:
                            h_ps[b, t, s] = bank(2 * t + s, f"h_ps{b}{t}{s}")
                        sensors = slice(BANK * s, BANK * (s + 1))
                        nc.tensor.matmul_mx(
                            out=h_ps[b, t, s][:],
                            lhsT=w_c[a, c, i].bitcast(FP8X4),
                            lhsT_scale=w_s[a, c, i],
                            rhs=v_w[a][:, sensors].bitcast(FP8X4),
                            rhs_scale=v_sc[4 * a : P, sensors],
                            start=(a == 0),
                            stop=(a == PASSES - 1),
                        )

        def copy_out(b, t, copy, over=None):
            h[b, t] = sb([P, S], F32, f"h{b}{t}", over)
            for s in range(2):
                copy(h[b, t][:, BANK * s : BANK * (s + 1)], h_ps[b, t, s][:])

        d_run = sb([P, 5 * RUN], F32, "d_run")
        z_t0 = [
            d_run[:, 3 * RUN : 5 * RUN].bitcast(BF16).rearrange("p (j x) -> p j x", j=4),
            sb([P, 4, RUN], BF16, "z_t0_1")[:],
        ]
        end_b1, diff1, z_t1, z_words, z_c, z_s, y_ps = {}, {}, {}, {}, {}, {}, {}
        factors, turned, b_turned, gated, res = {}, {}, {}, {}, {}

        def gather_b0(t):
            nc.vector.tensor_copy(end_b0[:, t, :], h[0, t][:].indirect(pos2_sb[:, :]))

        def gather_d0(t, first=0, count=NP):
            pairs = slice(first, first + count)
            picked = h[0, t][:].indirect(listed(pos1_sb, first, count))
            nc.vector.tensor_tensor(diff0[:, t, pairs], picked, end_b0[:, t, pairs], ALU.subtract)

        def weigh0(t, first=0, count=NP):
            pairs = slice(first, first + count)
            factor = gain0[:, t : t + 1]
            nc.gpsimd.tensor_scalar(weighed0[:, t, pairs], diff0[:, t, pairs], factor, 0.0, ALU.mult, ALU.add)

        def move_z0(c, i):
            for t in (2 * c, 2 * c + 1):
                nc.sync.dma_start(z_t0[i][32 * t : 32 * (t + 1), :, :], weighed0[:, t, RUN * i : RUN * (i + 1)])

        def gather_b1(q, t, over=None):
            if q not in end_b1:
                end_b1[q] = sb([P, 4, P], F32, f"end_b1_{q}", over)[:]
            nc.vector.tensor_copy(end_b1[q][:, t, :], h[1, t][:].indirect(listed(pos2_sb, P * q, P)))

        def gather_d1(q, t):
            if q not in diff1:
                diff1[q] = sb([P, 4, P], F32, f"diff1_{q}")[:]
            picked = h[1, t][:].indirect(listed(pos1_sb, P * q, P))
            nc.vector.tensor_tensor(diff1[q][:, t, :], picked, end_b1[q][:, t, :], ALU.subtract)

        def weigh1(q, t):
            if q not in z_t1:
                z_t1[q] = sb([P, 4, P], BF16, f"z_t1_{q}")[:]
            nc.scalar.activation(z_t1[q][:, t, :], diff1[q][:, t, :], ACT.Copy, scale=gain1[:, t : t + 1])

        def weigh_words(q):
            z_words[1, q] = sb([P, P, 4], BF16, f"z_words1{q}")
            factor = gain1[:].unsqueeze(1).to_broadcast([P, P, 4])
            nc.gpsimd.tensor_tensor(z_words[1, q][:], diff1[q].rearrange("p t x -> p x t"), factor, ALU.mult)

        def interleave(b, q, src):
            z_words[b, q] = sb([P, src.shape[2], 4], BF16, f"z_words{b}{q}")
            nc.scalar.copy(
                z_words[b, q][:].rearrange("p (x i) j -> p x j i", i=4), src.rearrange("p j (x i) -> p x j i", i=4)
            )

        def quantise_z(b, q):
            n = z_words[b, q].shape[1]
            codes, scales = sb([P, n], U32, f"z_c{b}{q}"), sb([P, n], U8, f"z_s{b}{q}")
            nc.vector.quantize_mx(
                out=codes[:].bitcast(FP8X4), scales=scales[:], in_=z_words[b, q][:].rearrange("p x j -> p (x j)")
            )
            for i in range(n // P):
                z_c[b, q + i], z_s[b, q + i] = codes[:, P * i : P * (i + 1)], scales[:, P * i : P * (i + 1)]

        def y_pass(q, b):
            if b == 0:
                for n in range(2):
                    y_ps[q, n] = bank(2 * q + n, f"y_ps{q}{n}")
            nc.tensor.matmul_mx(
                out=y_ps[q, 1][:],
                lhsT=z_c[b, q].bitcast(FP8X4),
                lhsT_scale=z_s[b, q],
                rhs=w4_w[:, b, 2 * BANK : 4 * BANK].bitcast(FP4X4),
                rhs_scale=w4_sc[:, b, P : 2 * P].bitcast(U8),
                start=(b == 0),
                stop=(b == 1),
            )
            for t in range(4):
                nc.tensor.matmul_mx(
                    out=y_ps[q, 0][:, P * t : P * (t + 1)],
                    lhsT=w4_w[:, b, 2 * P * t : 2 * P * (t + 1)].bitcast(FP4X4),
                    lhsT_scale=w4_sc[:, b, 32 * t : 32 * (t + 1)].bitcast(U8),
                    rhs=z_c[b, q].bitcast(FP8X4),
                    rhs_scale=z_s[b, q],
                    start=(b == 0 and t == 0),
                    stop=(b == 1 and t == 3),
                )

        def by_tile(ps):
            return ps[:].rearrange("p (t x) -> p t x", t=4)

        def turn(dst, src, first=True, last=True):
            for t in range(4):
                start, stop = (True, True) if first and last else (first and t == 0, last and t == 3)
                nc.tensor.matmul(dst[:, P * t : P * (t + 1)], src[:, t, :], ident[:], start, stop, is_transpose=True)

        def turn_b1(q, i, over=None):
            b_ps = bank(i, f"b_ps{q}")
            turn(b_ps, end_b1[q])
            b_turned[q] = sb([P, 4, P], F32, f"b_turned{q}", over)
            nc.scalar.activation(b_turned[q][:], by_tile(b_ps), ACT.Copy, scale=2.0)

        def gate(q):
            if q not in turned:
                turned[q] = sb([P, 4, P], F32, f"turned{q}")[:]
            nc.scalar.activation(turned[q], y_ps[q, 1][:].rearrange("p (m t) -> p t m", t=4), ACT.Tanh, scale=0.5)
            other_ps = bank(2 * q + 1, f"other_ps{q}")
            turn(other_ps, diff1[q] if q in SUMMED else turned[q])
            gate0 = sb([P, 4, P], F32, f"gate0_{q}")
            nc.scalar.activation(gate0[:], by_tile(y_ps[q, 0]), ACT.Tanh, scale=0.5)
            factors[q, 0] = (gate0[:], diff0[:, :, P * q : P * (q + 1)])
            factors[q, 1] = (turned[q], by_tile(other_ps)) if q in SUMMED else (by_tile(other_ps), diff1[q])

        def store(q, n):
            pairs = slice(P * q, P * (q + 1))
            if n == 0:
                rows = out[0:BANK, pairs].rearrange("(t p) x -> p t x", t=4)
            else:
                rows = out[BANK:H, pairs].rearrange("(p t) x -> p t x", t=4)
            nc.sync.dma_start(rows, res[q, n])

        def product(q, n):
            if (q, n) not in gated:
                gated[q, n] = sb([P, 4, P], F32, f"gated{q}{n}")[:]
            tanh, d = factors[q, n]
            nc.vector.scalar_tensor_tensor(gated[q, n], tanh, 1.0, d, ALU.add, ALU.mult)

        def add(q, n):
            res[q, n] = sb([P, 4, P], F32, f"res{q}{n}")[:]
            b = end_b1[q] if n else end_b0[:, :, P * q : P * (q + 1)]
            nc.vector.scalar_tensor_tensor(res[q, n], gated[q, n], 0.5, b, ALU.mult, ALU.add)
            store(q, n)

        def add_turned(q):
            sum_ps = bank(2 * q, f"sum_ps{q}")
            turn(sum_ps, b_turned[q], last=False)
            turn(sum_ps, gated[q, 1], first=False)
            if (q, 1) not in res:
                res[q, 1] = sb([P, 4, P], F32, f"res{q}1")[:]
            nc.scalar.activation(res[q, 1], by_tile(sum_ps), ACT.Copy, scale=0.5)
            store(q, 1)

        gather_table(0)
        nc.vector.tensor_copy(v_sc[:], tab_sc[:].bitcast(U8).indirect(offs_sb[:]))
        cast0(0, 0)
        quantise_w1(0, 0, 0, 2)
        gather_table(1)
        cast0(1, 0)
        quantise_w1(1, 0, 0, 2)
        gather_table(2)
        cast0(2, 0)
        quantise_w1(2, 0, 0, 1)
        quantise_w1(2, 0, 1, 2)
        states(0)

        cast0(0, 1, nc.vector.tensor_copy, "raw20")
        quantise_w1(0, 1, 0, 2)
        copy_out(0, 0, nc.vector.tensor_copy)
        cast0(1, 1)
        copy_out(0, 1, nc.scalar.copy, "raw11")
        cast0(2, 1)
        gather_b0(0)
        quantise_w1(1, 1, 0, 2)
        gather_d0(0)
        cast1(0, 2)
        cast1(0, 3)
        quantise_w1(2, 1, 0, 2)
        states(1)
        weigh0(0)

        gather_b0(1)
        quantise_w1(0, HALF1, 0, 4)
        gather_d0(1)
        weigh0(1)
        for i in range(2):
            move_z0(0, i)
        cast1(1, 2)
        copy_out(0, 2, nc.scalar.copy, "raw12")
        cast1(1, 3)

        gather_b0(2)
        cast1(2, 3, nc.vector.tensor_copy, 0, 2)
        cast1(2, 2)
        copy_out(0, 3, nc.scalar.copy, "raw22")
        cast1(2, 3, nc.scalar.copy, 2, 4)
        quantise_w1(1, HALF1, 0, 4)
        gather_d0(2)
        weigh0(2)

        quantise_w1(2, HALF1, 0, 1)
        gather_b0(3)
        quantise_w1(2, HALF1, 1, 2)
        quantise_w1(2, HALF1, 2, 4)
        states(HALF1)
        for i in range(2):
            gather_d0(3, RUN * i, RUN)
            weigh0(3, RUN * i, RUN)
            move_z0(1, i)

        for t, over in enumerate(("tab_w0", "tab_w1", "tab_w2", "h00")):
            copy_out(1, t, nc.scalar.copy, over)
        interleave(0, 0, z_t0[0])
        interleave(0, 2, z_t0[1])

        diff1[2] = sb([P, 4, P], F32, "diff1_2", "z_room")[:]
        z_t1[0] = diff1[2].bitcast(BF16)[:, :, 0:P]

        for q in range(2):
            diff1[q] = d_run[:, 0 : 4 * RUN].rearrange("p (t x) -> p t x", t=4)[:, :, P * q : P * (q + 1)]
        room3 = sb([P, 4 * BANK], F32, "room3")[:]
        z_t1[3] = room3.rearrange("p (t x) -> p t x", t=4).bitcast(BF16)[:, :, 0:P]
        part3 = room3.rearrange("p (i t x) -> p i t x", i=4, t=4)
        gated[1, 0], gated[1, 1], turned[2], res[0, 1] = (part3[:, i, :, :] for i in range(4))

        for t in range(4):
            gather_b1(0, t)
            gather_b1(1, t)
            if t == 3:
                quantise_z(0, 0)
            gather_d1(0, t)
            gather_d1(1, t)
        weigh_words(1)
        for t in range(4):
            weigh1(0, t)
        quantise_z(0, 2)
        y_pass(0, 0)
        y_pass(1, 0)
        turn_b1(0, 4, "z_words00")
        interleave(1, 0, z_t1[0])
        turn_b1(1, 6, "z_words02")
        for t in range(4):
            gather_b1(2, t, over="z_t0_1")
        turn_b1(2, 4)
        quantise_z(1, 0)
        y_pass(0, 1)
        quantise_z(1, 1)
        y_pass(1, 1)
        for t in range(4):
            gather_d1(2, t)
        weigh_words(2)
        y_pass(2, 0)
        y_pass(3, 0)
        gate(0)
        for t in range(4):
            gather_b1(3, t, over="z_words10")
        for t in range(4):
            gather_d1(3, t)
        gate(1)
        quantise_z(1, 2)
        y_pass(2, 1)
        for t in range(4):
            weigh1(3, t)
        interleave(1, 3, z_t1[3])
        gate(2)

        part2 = sb([P, 2 * BANK], F32, "gated0", "z_words12")[:].rearrange("p (i t x) -> p i t x", i=2, t=4)
        gated[0, 0], gated[0, 1] = part2[:, 0, :, :], part2[:, 1, :, :]
        product(0, 1)
        product(0, 0)
        add(0, 0)
        quantise_z(1, 3)
        y_pass(3, 1)
        gate(3)
        for q in range(1, 4):
            product(q, 1)
            product(q, 0)
            if q == 3:
                add(q, 1)
            add(q, 0)
        add_turned(0)
        add_turned(1)
        add_turned(2)
